import numpy as np
import ml_dtypes


def mxq(x, axis, fmt="e4m3"):
    dtype, down = {"e4m3": (ml_dtypes.float8_e4m3fn, 7), "e5m2": (ml_dtypes.float8_e5m2, 14)}[fmt]
    v = np.moveaxis(np.asarray(x, np.float32).astype(ml_dtypes.bfloat16).astype(np.float64), axis, -1)
    blocks = v.reshape(v.shape[:-1] + (-1, 32))
    amax = np.abs(blocks).max(-1, keepdims=True)
    byte = np.maximum(np.where(amax > 0, np.frexp(amax)[1] - 1 + 127, 0) - down, 1)
    scale = np.exp2(byte - 127.0)
    codes = (blocks / scale).astype(np.float32).astype(dtype).astype(np.float64)
    return np.moveaxis((codes * scale).reshape(v.shape), -1, axis)


WIDE = False


def mx_kscale(k):
    if not WIDE:
        return np.ones(k)
    levels = np.array([10, -10, 5, -5, 0])
    if k % 512:
        return np.exp2(np.random.permutation(np.resize(levels, k // 32))).repeat(32)
    a = np.empty((k // 512, 16))
    for p in range(k // 512):
        a[p, :8] = np.random.permutation(np.resize(levels, 8))
        for g in range(8):
            far = levels[np.abs(levels - a[p, g]) >= 10]
            a[p, g + 8] = far[np.random.randint(len(far))]
    return np.exp2(a.ravel()).repeat(32)


def f64(x):
    return np.asarray(x).astype(np.float64)


def striped(idx):
    return np.tile(idx.reshape(-1, 16).T, (8, 1)).astype(np.uint16)


def unstriped(offs):
    return offs[:16].T.reshape(-1).astype(np.int64)


def pack_weight(w):
    k, n = w.shape
    w = f64(np.asarray(w, np.float32).astype(ml_dtypes.bfloat16)).reshape(k // 32, 32, n)
    amax = np.abs(w).max(1)
    byte = np.clip(np.where(amax > 0, np.frexp(amax)[1] - 1 + 127 - 7, 1), 1, 254)
    scaled = (w * np.exp2(127.0 - byte)[:, None, :]).reshape(k, n).astype(np.float32)
    words = np.ascontiguousarray(scaled.reshape(k // 512, 128, 4, n).transpose(0, 1, 3, 2)).astype(ml_dtypes.float8_e4m3fn).view(np.uint8)
    return words, np.ascontiguousarray(byte.astype(np.uint8).reshape(k // 512, 16, n))


def unpack_weight(words, scales):
    g, p, n, _ = words.shape
    vals = np.ascontiguousarray(words).view(ml_dtypes.float8_e4m3fn).astype(np.float64) * np.repeat(np.exp2(scales.astype(np.float64) - 127.0), 8, axis=1)[..., None]
    return vals.transpose(0, 1, 3, 2).reshape(g * 512, n)


K, T, S, N, U = 1024, 1024, 512, 128, 1024
P = 2 ** 7


def setup_inputs():
    n = np.random.standard_normal
    s = mx_kscale(K)[:, None]
    packed_w1 = pack_weight(n((K, N)) / np.sqrt(K) / s)
    return {
        "xT": (n((K, T)) * s).astype(np.float32),
        "mem": n((N, U)).astype(np.float32),
        "w1_words": packed_w1[0],
        "w1_scales": packed_w1[1],
        "old": np.tile(np.random.uniform(0.5, 0.95, S), (P, 1)).astype(np.float32),
        "new": np.tile(np.random.uniform(0.05, 0.5, S), (P, 1)).astype(np.float32),
        "offs": striped(np.random.permutation(T)[:S]),
        "slot": striped(np.random.permutation(U)[:S]),
    }


def reference(xT, mem, w1_words, w1_scales, old, new, offs, slot):
    xq = mxq(f64(xT)[:, unstriped(offs)], 0, "e4m3")
    y = np.tanh(unpack_weight(w1_words, w1_scales).T @ xq)
    out = f64(mem).copy()
    out[:, unstriped(slot)] = f64(mem)[:, unstriped(slot)] * f64(old)[:1] + y * f64(new)[:1]
    return out

@@ -1,0 +1,182 @@
+from contextlib import ExitStack
+
+import concourse.mybir as mybir
+from concourse.masks import make_identity
+
+K, T, S, N, U = 1024, 1024, 512, 128, 1024
+FLOPS = 2 * K * N * S
+
+F32 = mybir.dt.float32
+BF16 = mybir.dt.bfloat16
+I32 = mybir.dt.int32
+U32 = mybir.dt.uint32
+U16 = mybir.dt.uint16
+U8 = mybir.dt.uint8
+FP8X4 = mybir.dt.float8_e4m3fn_x4
+MULT = mybir.AluOpType.mult
+ADD = mybir.AluOpType.add
+TANH = mybir.ActivationFunctionType.Tanh
+
+P = 128
+PASSES = 2
+HALF = T // 2
+FRONT = [(0, 128), (128, 256), (256, 384), (384, 512)]
+BACK = [(0, 128), (128, 256), (256, 512)]
+VECTOR_COLS = [320, 320, 320, 320]
+
+
+def tile_picked_ema_tanh_e_kernel(
+    tc, xT, mem, w1_words, w1_scales, old, new, offs, slot, out
+):
+    nc = tc.nc
+    with ExitStack() as ctx:
+        sb = ctx.enter_context(tc.tile_pool(name="sb", bufs=1))
+        ps = ctx.enter_context(tc.psum_pool(name="ps", bufs=1))
+
+        offs_t = sb.tile([P, S // 16], U16, name="offs_t")
+        slot_t = sb.tile([P, S // 16], U16, name="slot_t")
+        mem_t = sb.tile([P, U], F32, name="mem_t")
+        old_col = sb.tile([P, 4], F32, name="old_col")
+        new_col = sb.tile([P, 4], F32, name="new_col")
+        ident = sb.tile([P, P], F32, name="ident")
+        w_words = sb.tile([P, PASSES, N], U32, name="w_words", align_bytes=64)
+        w_scales = sb.tile([P, PASSES, N], U8, name="w_scales", align_bytes=64)
+        warm_in = sb.tile([P, 1], F32, name="warm_in")
+        warm_out = sb.tile([P, 1], F32, name="warm_out")
+
+        nc.scalar.dma_start(out=old_col[:], in_=old[0].rearrange("(p c) -> p c", c=4))
+        nc.scalar.dma_start(out=new_col[:], in_=new[0].rearrange("(p c) -> p c", c=4))
+        nc.vector.memset(w_scales[:].bitcast(I32), 0)
+        nc.vector.memset(warm_in[:], 0.0)
+        nc.scalar.activation(warm_out[:], warm_in[:], TANH)
+
+        x_rows = xT.rearrange("(z p u e) t -> z u p e t", z=PASSES, p=P, u=2, e=2)
+        raw = {}
+
+        def load_half(z, u, h):
+            t = sb.tile([P, 2, HALF], F32, name="raw%d%d%d" % (z, u, h))
+            nc.sync.dma_start(out=t[:], in_=x_rows[z, u, :, :, h * HALF : (h + 1) * HALF])
+            raw[z, u, h] = t
+
+        nc.sync.dma_start(out=mem_t[:], in_=mem)
+        nc.sync.dma_start(slot_t[:], slot)
+        load_half(0, 0, 0)
+        nc.sync.dma_start(offs_t[:], offs)
+        load_half(0, 0, 1)
+        load_half(0, 1, 0)
+        load_half(0, 1, 1)
+        for q in range(4):
+            nc.sync.dma_start(
+                out=w_scales[32 * q : 32 * q + 4, :, :].bitcast(I32),
+                in_=w1_scales[:, 4 * q : 4 * q + 4, :].rearrange("z r n -> r z n").bitcast(I32),
+            )
+        for u in range(2):
+            for h in range(2):
+                load_half(1, u, h)
+        nc.sync.dma_start(
+            out=w_words[:].bitcast(I32),
+            in_=w1_words.rearrange("z p n t -> p z (n t)").bitcast(I32),
+        )
+
+        make_identity(nc, ident[:])
+
+        old_ps = ps.tile([P, 4, P], F32, name="old_ps")
+        new_ps = ps.tile([P, 4, P], F32, name="new_ps")
+        for col, dst in ((old_col, old_ps), (new_col, new_ps)):
+            for c in range(4):
+                nc.tensor.transpose(dst[:, c, :], col[:, c : c + 1].to_broadcast([P, P]), ident[:])
+
+        mem_picked = sb.tile([P, S], F32, name="mem_picked")
+        kept = sb.tile([P, S], F32, name="kept")
+        nc.vector.tensor_copy(mem_picked[:], mem_t[:].indirect(slot_t[:]))
+        nc.vector.tensor_tensor(
+            kept[:].rearrange("p (t c) -> p t c", c=4),
+            mem_picked[:].rearrange("p (t c) -> p t c", c=4),
+            old_ps[:].rearrange("p c t -> p t c"),
+            MULT,
+        )
+
+        def cast(engine_copy, pairs, z, u, h, a, b):
+            engine_copy(
+                pairs[:, h * HALF + a : h * HALF + b, :],
+                raw[z, u, h][:, :, a:b].rearrange("p e t -> p t e"),
+            )
+
+        def make_pairs(z, u, vector_cols):
+            pairs = sb.tile([P, T, 2], BF16, name="pairs%d%d" % (z, u), align_bytes=64)
+            cast(nc.scalar.copy, pairs, z, u, 0, 0, HALF)
+            if vector_cols < HALF:
+                cast(nc.scalar.copy, pairs, z, u, 1, vector_cols, HALF)
+            if vector_cols > 0:
+                cast(nc.vector.tensor_copy, pairs, z, u, 1, 0, vector_cols)
+            return pairs[:].rearrange("p t e -> p (t e)").bitcast(U32)
+
+        def quantise(woven, z, a, b):
+            codes = sb.tile([P, b - a], U32, name="codes%d_%d" % (z, a), align_bytes=64)
+            scales = sb.tile([P, b - a], U8, name="scales%d_%d" % (z, a), align_bytes=64)
+            nc.vector.quantize_mx(
+                out=codes[:].bitcast(FP8X4),
+                scales=scales[:],
+                in_=woven[:].rearrange("p j u -> p (j u)").bitcast(BF16),
+            )
+            return codes, scales
+
+        def product(acc, z, codes, scales):
+            nc.tensor.matmul_mx(
+                out=acc[:],
+                lhsT=w_words[:, z, :].bitcast(FP8X4),
+                lhsT_scale=w_scales[:, z, :],
+                rhs=codes.bitcast(FP8X4),
+                rhs_scale=scales,
+                start=(z == 0),
+                stop=(z == PASSES - 1),
+            )
+
+        front = FRONT
+        back = BACK
+        accs = [ps.tile([P, b - a], F32, name="acc%d" % a) for a, b in front]
+
+        woven0 = sb.tile([P, S, 2], U32, name="woven0", align_bytes=64)
+        for u in range(2):
+            window = make_pairs(0, u, VECTOR_COLS[u])
+            nc.vector.tensor_copy(woven0[:, :, u], window.indirect(offs_t[:]))
+        codes0, scales0 = quantise(woven0, 0, 0, S)
+        for c, (a, b) in enumerate(front):
+            product(accs[c], 0, codes0[:, a:b], scales0[:, a:b])
+
+        woven1 = [sb.tile([P, b - a, 2], U32, name="woven1_%d" % a, align_bytes=64) for a, b in front]
+        window = make_pairs(1, 0, VECTOR_COLS[2])
+        for c, (a, b) in enumerate(front):
+            nc.vector.tensor_copy(woven1[c][:, :, 0], window.indirect(offs_t[:, a // 16 : b // 16]))
+        window = make_pairs(1, 1, VECTOR_COLS[3])
+        for c, (a, b) in enumerate(front):
+            nc.vector.tensor_copy(woven1[c][:, :, 1], window.indirect(offs_t[:, a // 16 : b // 16]))
+            codes, scales = quantise(woven1[c], 1, a, b)
+            product(accs[c], 1, codes[:], scales[:])
+        ys = [sb.tile([P, b - a], F32, name="y%d" % a) for a, b in back]
+        for c, (a, b) in enumerate(front):
+            g = max(i for i in range(len(back)) if back[i][0] <= a)
+            nc.scalar.activation(ys[g][:, a - back[g][0] : b - back[g][0]], accs[c][:], TANH)
+        moved = [sb.tile([P, b - a], F32, name="moved%d" % a) for a, b in back]
+
+        def scale_new(g):
+            a, b = back[g]
+            nc.vector.tensor_tensor(
+                moved[g][:].rearrange("p (t c) -> p t c", c=4),
+                ys[g][:].rearrange("p (t c) -> p t c", c=4),
+                new_ps[:, :, a // 4 : b // 4].rearrange("p c t -> p t c"),
+                MULT,
+            )
+
+        def put(g):
+            a, b = back[g]
+            nc.vector.tensor_tensor(
+                mem_t[:].indirect(slot_t[:, a // 16 : b // 16]), moved[g][:], kept[:, a:b], ADD
+            )
+
+        scale_new(0)
+        for g in range(len(back)):
+            if g + 1 < len(back):
+                scale_new(g + 1)
+            put(g)
+        nc.sync.dma_start(out=out, in_=mem_t[:])

@@ -22,7 +22,8 @@ PASSES = 2
 HALF = T // 2
 FRONT = [(0, 128), (128, 256), (256, 384), (384, 512)]
 BACK = [(0, 128), (128, 256), (256, 512)]
-VECTOR_COLS = [320, 320, 320, 320]
+PASS0 = [(0, 256, "raw100"), (256, 512, "raw110")]
+VECTOR_COLS = [320, 320, 320, 384]
 
 
 def tile_picked_ema_tanh_e_kernel(
@@ -54,7 +55,7 @@ def tile_picked_ema_tanh_e_kernel(
         raw = {}
 
         def load_half(z, u, h):
-            t = sb.tile([P, 2, HALF], F32, name="raw%d%d%d" % (z, u, h))
+            t = sb.tile([P, 2, HALF], F32, name="raw%d%d%d" % (z, u, h), tag="raw%d%d%d" % (z, u, h), align_bytes=64)
             nc.sync.dma_start(out=t[:], in_=x_rows[z, u, :, :, h * HALF : (h + 1) * HALF])
             raw[z, u, h] = t
 
@@ -65,11 +66,6 @@ def tile_picked_ema_tanh_e_kernel(
         load_half(0, 0, 1)
         load_half(0, 1, 0)
         load_half(0, 1, 1)
-        for q in range(4):
-            nc.sync.dma_start(
-                out=w_scales[32 * q : 32 * q + 4, :, :].bitcast(I32),
-                in_=w1_scales[:, 4 * q : 4 * q + 4, :].rearrange("z r n -> r z n").bitcast(I32),
-            )
         for u in range(2):
             for h in range(2):
                 load_half(1, u, h)
@@ -77,6 +73,11 @@ def tile_picked_ema_tanh_e_kernel(
             out=w_words[:].bitcast(I32),
             in_=w1_words.rearrange("z p n t -> p z (n t)").bitcast(I32),
         )
+        for q in range(4):
+            nc.sync.dma_start(
+                out=w_scales[32 * q : 32 * q + 4, :, :].bitcast(I32),
+                in_=w1_scales[:, 4 * q : 4 * q + 4, :].rearrange("z r n -> r z n").bitcast(I32),
+            )
 
         make_identity(nc, ident[:])
 
@@ -86,6 +87,8 @@ def tile_picked_ema_tanh_e_kernel(
             for c in range(4):
                 nc.tensor.transpose(dst[:, c, :], col[:, c : c + 1].to_broadcast([P, P]), ident[:])
 
+        new_row = sb.tile([P, S], F32, name="new_row")
+        nc.scalar.copy(new_row[:].rearrange("p (t c) -> p t c", c=4), new_ps[:].rearrange("p c t -> p t c"))
         mem_picked = sb.tile([P, S], F32, name="mem_picked")
         kept = sb.tile([P, S], F32, name="kept")
         nc.vector.tensor_copy(mem_picked[:], mem_t[:].indirect(slot_t[:]))
@@ -111,13 +114,13 @@ def tile_picked_ema_tanh_e_kernel(
                 cast(nc.vector.tensor_copy, pairs, z, u, 1, 0, vector_cols)
             return pairs[:].rearrange("p t e -> p (t e)").bitcast(U32)
 
-        def quantise(woven, z, a, b):
-            codes = sb.tile([P, b - a], U32, name="codes%d_%d" % (z, a), align_bytes=64)
+        def quantise(woven, z, a, b, tag):
+            codes = sb.tile([P, b - a], U32, name="codes%d_%d" % (z, a), tag=tag, align_bytes=64)
             scales = sb.tile([P, b - a], U8, name="scales%d_%d" % (z, a), align_bytes=64)
             nc.vector.quantize_mx(
                 out=codes[:].bitcast(FP8X4),
                 scales=scales[:],
-                in_=woven[:].rearrange("p j u -> p (j u)").bitcast(BF16),
+                in_=woven.rearrange("p j u -> p (j u)").bitcast(BF16),
             )
             return codes, scales
 
@@ -136,22 +139,32 @@ def tile_picked_ema_tanh_e_kernel(
         back = BACK
         accs = [ps.tile([P, b - a], F32, name="acc%d" % a) for a, b in front]
 
-        woven0 = sb.tile([P, S, 2], U32, name="woven0", align_bytes=64)
+        woven0 = [sb.tile([P, b - a, 2], U32, name="woven0_%d" % a, align_bytes=64) for a, b, tag in PASS0]
         for u in range(2):
             window = make_pairs(0, u, VECTOR_COLS[u])
-            nc.vector.tensor_copy(woven0[:, :, u], window.indirect(offs_t[:]))
-        codes0, scales0 = quantise(woven0, 0, 0, S)
-        for c, (a, b) in enumerate(front):
-            product(accs[c], 0, codes0[:, a:b], scales0[:, a:b])
+            for c, (a, b, tag) in enumerate(PASS0):
+                nc.vector.tensor_copy(woven0[c][:, :, u], window.indirect(offs_t[:, a // 16 : b // 16]))
 
-        woven1 = [sb.tile([P, b - a, 2], U32, name="woven1_%d" % a, align_bytes=64) for a, b in front]
-        window = make_pairs(1, 0, VECTOR_COLS[2])
+        def first_pass(piece):
+            a0, b0, tag = PASS0[piece]
+            codes0, scales0 = quantise(woven0[piece][:], 0, a0, b0, tag)
+            for c, (a, b) in enumerate(front):
+                if a0 <= a < b0:
+                    product(accs[c], 0, codes0[:, a - a0 : b - a0], scales0[:, a - a0 : b - a0])
+
+        picked1 = [sb.tile([P, 2, b - a], U32, name="picked1_%d" % a) for a, b in front]
+        for u in range(2):
+            window = make_pairs(1, u, VECTOR_COLS[2 + u])
+            first_pass(u)
+            for c, (a, b) in enumerate(front):
+                nc.vector.tensor_copy(picked1[c][:, u, :], window.indirect(offs_t[:, a // 16 : b // 16]))
+        woven1 = []
         for c, (a, b) in enumerate(front):
-            nc.vector.tensor_copy(woven1[c][:, :, 0], window.indirect(offs_t[:, a // 16 : b // 16]))
-        window = make_pairs(1, 1, VECTOR_COLS[3])
+            woven = sb.tile([P, b - a, 2], U32, name="woven1_%d" % a, align_bytes=64)
+            nc.scalar.copy(woven[:], picked1[c][:].rearrange("p u j -> p j u"))
+            woven1.append(woven)
         for c, (a, b) in enumerate(front):
-            nc.vector.tensor_copy(woven1[c][:, :, 1], window.indirect(offs_t[:, a // 16 : b // 16]))
-            codes, scales = quantise(woven1[c], 1, a, b)
+            codes, scales = quantise(woven1[c][:], 1, a, b, "codes1_%d" % a)
             product(accs[c], 1, codes[:], scales[:])
         ys = [sb.tile([P, b - a], F32, name="y%d" % a) for a, b in back]
         for c, (a, b) in enumerate(front):
@@ -161,12 +174,7 @@ def tile_picked_ema_tanh_e_kernel(
 
         def scale_new(g):
             a, b = back[g]
-            nc.vector.tensor_tensor(
-                moved[g][:].rearrange("p (t c) -> p t c", c=4),
-                ys[g][:].rearrange("p (t c) -> p t c", c=4),
-                new_ps[:, :, a // 4 : b // 4].rearrange("p c t -> p t c"),
-                MULT,
-            )
+            nc.vector.tensor_tensor(moved[g][:], ys[g][:], new_row[:, a:b], MULT)
 
         def put(g):
             a, b = back[g]

@@ -1,7 +1,6 @@
 from contextlib import ExitStack
 
 import concourse.mybir as mybir
-from concourse.masks import make_identity
 
 K, T, S, N, U = 1024, 1024, 512, 128, 1024
 FLOPS = 2 * K * N * S
@@ -21,9 +20,10 @@ P = 128
 PASSES = 2
 HALF = T // 2
 FRONT = [(0, 128), (128, 256), (256, 384), (384, 512)]
-BACK = [(0, 128), (128, 256), (256, 512)]
-PASS0 = [(0, 256, "raw100"), (256, 512, "raw110")]
-VECTOR_COLS = [320, 320, 320, 384]
+BACK = [(0, 128), (128, 512)]
+PASS0 = [(0, 256, "raw101"), (256, 512, "raw110")]
+KEPT_TAGS = ["woven1_256", "woven1_384"]
+VECTOR_COLS = [320, 320, 256, 352]
 
 
 def tile_picked_ema_tanh_e_kernel(
@@ -37,16 +37,13 @@ def tile_picked_ema_tanh_e_kernel(
         offs_t = sb.tile([P, S // 16], U16, name="offs_t")
         slot_t = sb.tile([P, S // 16], U16, name="slot_t")
         mem_t = sb.tile([P, U], F32, name="mem_t")
-        old_col = sb.tile([P, 4], F32, name="old_col")
-        new_col = sb.tile([P, 4], F32, name="new_col")
-        ident = sb.tile([P, P], F32, name="ident")
+        old_row = sb.tile([P, S], F32, name="old_row")
+        new_row = sb.tile([P, S], F32, name="new_row")
         w_words = sb.tile([P, PASSES, N], U32, name="w_words", align_bytes=64)
         w_scales = sb.tile([P, PASSES, N], U8, name="w_scales", align_bytes=64)
         warm_in = sb.tile([P, 1], F32, name="warm_in")
         warm_out = sb.tile([P, 1], F32, name="warm_out")
 
-        nc.scalar.dma_start(out=old_col[:], in_=old[0].rearrange("(p c) -> p c", c=4))
-        nc.scalar.dma_start(out=new_col[:], in_=new[0].rearrange("(p c) -> p c", c=4))
         nc.vector.memset(w_scales[:].bitcast(I32), 0)
         nc.vector.memset(warm_in[:], 0.0)
         nc.scalar.activation(warm_out[:], warm_in[:], TANH)
@@ -59,8 +56,6 @@ def tile_picked_ema_tanh_e_kernel(
             nc.sync.dma_start(out=t[:], in_=x_rows[z, u, :, :, h * HALF : (h + 1) * HALF])
             raw[z, u, h] = t
 
-        nc.sync.dma_start(out=mem_t[:], in_=mem)
-        nc.sync.dma_start(slot_t[:], slot)
         load_half(0, 0, 0)
         nc.sync.dma_start(offs_t[:], offs)
         load_half(0, 0, 1)
@@ -78,41 +73,25 @@ def tile_picked_ema_tanh_e_kernel(
                 out=w_scales[32 * q : 32 * q + 4, :, :].bitcast(I32),
                 in_=w1_scales[:, 4 * q : 4 * q + 4, :].rearrange("z r n -> r z n").bitcast(I32),
             )
-
-        make_identity(nc, ident[:])
-
-        old_ps = ps.tile([P, 4, P], F32, name="old_ps")
-        new_ps = ps.tile([P, 4, P], F32, name="new_ps")
-        for col, dst in ((old_col, old_ps), (new_col, new_ps)):
-            for c in range(4):
-                nc.tensor.transpose(dst[:, c, :], col[:, c : c + 1].to_broadcast([P, P]), ident[:])
-
-        new_row = sb.tile([P, S], F32, name="new_row")
-        nc.scalar.copy(new_row[:].rearrange("p (t c) -> p t c", c=4), new_ps[:].rearrange("p c t -> p t c"))
-        mem_picked = sb.tile([P, S], F32, name="mem_picked")
-        kept = sb.tile([P, S], F32, name="kept")
-        nc.vector.tensor_copy(mem_picked[:], mem_t[:].indirect(slot_t[:]))
-        nc.vector.tensor_tensor(
-            kept[:].rearrange("p (t c) -> p t c", c=4),
-            mem_picked[:].rearrange("p (t c) -> p t c", c=4),
-            old_ps[:].rearrange("p c t -> p t c"),
-            MULT,
-        )
+        nc.sync.dma_start(slot_t[:], slot)
+        nc.sync.dma_start(out=mem_t[:], in_=mem)
+        nc.sync.dma_start(out=old_row[:], in_=old)
+        nc.sync.dma_start(out=new_row[:], in_=new)
 
         def cast(engine_copy, pairs, z, u, h, a, b):
             engine_copy(
-                pairs[:, h * HALF + a : h * HALF + b, :],
+                pairs[:, 2 * (h * HALF + a) : 2 * (h * HALF + b)].rearrange("p (t e) -> p t e", e=2),
                 raw[z, u, h][:, :, a:b].rearrange("p e t -> p t e"),
             )
 
         def make_pairs(z, u, vector_cols):
-            pairs = sb.tile([P, T, 2], BF16, name="pairs%d%d" % (z, u), align_bytes=64)
+            pairs = sb.tile([P, 2 * T], BF16, name="pairs%d%d" % (z, u), align_bytes=64)
             cast(nc.scalar.copy, pairs, z, u, 0, 0, HALF)
             if vector_cols < HALF:
                 cast(nc.scalar.copy, pairs, z, u, 1, vector_cols, HALF)
             if vector_cols > 0:
                 cast(nc.vector.tensor_copy, pairs, z, u, 1, 0, vector_cols)
-            return pairs[:].rearrange("p t e -> p (t e)").bitcast(U32)
+            return pairs[:].bitcast(U32)
 
         def quantise(woven, z, a, b, tag):
             codes = sb.tile([P, b - a], U32, name="codes%d_%d" % (z, a), tag=tag, align_bytes=64)
@@ -145,6 +124,7 @@ def tile_picked_ema_tanh_e_kernel(
             for c, (a, b, tag) in enumerate(PASS0):
                 nc.vector.tensor_copy(woven0[c][:, :, u], window.indirect(offs_t[:, a // 16 : b // 16]))
 
+
         def first_pass(piece):
             a0, b0, tag = PASS0[piece]
             codes0, scales0 = quantise(woven0[piece][:], 0, a0, b0, tag)
@@ -155,12 +135,15 @@ def tile_picked_ema_tanh_e_kernel(
         picked1 = [sb.tile([P, 2, b - a], U32, name="picked1_%d" % a) for a, b in front]
         for u in range(2):
             window = make_pairs(1, u, VECTOR_COLS[2 + u])
-            first_pass(u)
+            if u == 1:
+                first_pass(1)
             for c, (a, b) in enumerate(front):
                 nc.vector.tensor_copy(picked1[c][:, u, :], window.indirect(offs_t[:, a // 16 : b // 16]))
+            if u == 0:
+                first_pass(0)
         woven1 = []
         for c, (a, b) in enumerate(front):
-            woven = sb.tile([P, b - a, 2], U32, name="woven1_%d" % a, align_bytes=64)
+            woven = sb.tile([P, b - a, 2], U32, name="woven1_%d" % a, tag="woven1_%d" % a, align_bytes=64)
             nc.scalar.copy(woven[:], picked1[c][:].rearrange("p u j -> p j u"))
             woven1.append(woven)
         for c, (a, b) in enumerate(front):
@@ -170,21 +153,23 @@ def tile_picked_ema_tanh_e_kernel(
         for c, (a, b) in enumerate(front):
             g = max(i for i in range(len(back)) if back[i][0] <= a)
             nc.scalar.activation(ys[g][:, a - back[g][0] : b - back[g][0]], accs[c][:], TANH)
-        moved = [sb.tile([P, b - a], F32, name="moved%d" % a) for a, b in back]
+        moved = [old_row[:, a:b] for a, b in back]
 
         def scale_new(g):
             a, b = back[g]
-            nc.vector.tensor_tensor(moved[g][:], ys[g][:], new_row[:, a:b], MULT)
+            nc.vector.tensor_tensor(moved[g], ys[g][:], new_row[:, a:b], MULT)
+
+        kept = [sb.tile([P, b - a], F32, name="kept%d" % a, tag=KEPT_TAGS[g], align_bytes=64) for g, (a, b) in enumerate(back)]
+
+        def scale_old(g):
+            a, b = back[g]
+            nc.vector.tensor_tensor(kept[g][:], mem_t[:].indirect(slot_t[:, a // 16 : b // 16]), old_row[:, a:b], MULT)
 
         def put(g):
             a, b = back[g]
-            nc.vector.tensor_tensor(
-                mem_t[:].indirect(slot_t[:, a // 16 : b // 16]), moved[g][:], kept[:, a:b], ADD
-            )
+            nc.vector.tensor_tensor(mem_t[:].indirect(slot_t[:, a // 16 : b // 16]), moved[g], kept[g][:], ADD)
 
-        scale_new(0)
-        for g in range(len(back)):
-            if g + 1 < len(back):
-                scale_new(g + 1)
-            put(g)
+        for step in (scale_old, scale_new, put):
+            for g in range(len(back)):
+                step(g)
         nc.sync.dma_start(out=out, in_=mem_t[:])

@@ -21,7 +21,7 @@ PASSES = 2
 HALF = T // 2
 FRONT = [(0, 128), (128, 256), (256, 384), (384, 512)]
 BACK = [(0, 128), (128, 512)]
-PASS0 = [(0, 256, "raw101"), (256, 512, "raw110")]
+PASS0 = [(0, 256, "raw100"), (256, 512, "raw110")]
 KEPT_TAGS = ["woven1_256", "woven1_384"]
 VECTOR_COLS = [320, 320, 256, 352]
 
@@ -118,16 +118,16 @@ def tile_picked_ema_tanh_e_kernel(
         back = BACK
         accs = [ps.tile([P, b - a], F32, name="acc%d" % a) for a, b in front]
 
-        woven0 = [sb.tile([P, b - a, 2], U32, name="woven0_%d" % a, align_bytes=64) for a, b, tag in PASS0]
+        picked0 = sb.tile([P, 2, S], U32, name="picked0")
         for u in range(2):
             window = make_pairs(0, u, VECTOR_COLS[u])
-            for c, (a, b, tag) in enumerate(PASS0):
-                nc.vector.tensor_copy(woven0[c][:, :, u], window.indirect(offs_t[:, a // 16 : b // 16]))
-
+            nc.vector.tensor_copy(picked0[:, u, :], window.indirect(offs_t[:]))
 
         def first_pass(piece):
             a0, b0, tag = PASS0[piece]
-            codes0, scales0 = quantise(woven0[piece][:], 0, a0, b0, tag)
+            woven = sb.tile([P, b0 - a0, 2], U32, name="woven0_%d" % a0, tag=tag, align_bytes=64)
+            nc.scalar.copy(woven[:], picked0[:, :, a0:b0].rearrange("p u j -> p j u"))
+            codes0, scales0 = quantise(woven[:], 0, a0, b0, "codes0_%d" % a0)
             for c, (a, b) in enumerate(front):
                 if a0 <= a < b0:
                     product(accs[c], 0, codes0[:, a - a0 : b - a0], scales0[:, a - a0 : b - a0])
@@ -135,12 +135,9 @@ def tile_picked_ema_tanh_e_kernel(
         picked1 = [sb.tile([P, 2, b - a], U32, name="picked1_%d" % a) for a, b in front]
         for u in range(2):
             window = make_pairs(1, u, VECTOR_COLS[2 + u])
-            if u == 1:
-                first_pass(1)
             for c, (a, b) in enumerate(front):
                 nc.vector.tensor_copy(picked1[c][:, u, :], window.indirect(offs_t[:, a // 16 : b // 16]))
-            if u == 0:
-                first_pass(0)
+            first_pass(u)
         woven1 = []
         for c, (a, b) in enumerate(front):
             woven = sb.tile([P, b - a, 2], U32, name="woven1_%d" % a, tag="woven1_%d" % a, align_bytes=64)

@@ -18,12 +18,10 @@ TANH = mybir.ActivationFunctionType.Tanh
 
 P = 128
 PASSES = 2
-HALF = T // 2
-FRONT = [(0, 128), (128, 256), (256, 384), (384, 512)]
-BACK = [(0, 128), (128, 512)]
-PASS0 = [(0, 256, "raw100"), (256, 512, "raw110")]
-KEPT_TAGS = ["woven1_256", "woven1_384"]
-VECTOR_COLS = [320, 320, 256, 352]
+LOADS = [[(512, 512), (512, 192)], [(512, 512), (512, 192)], [(304, 304), (448, 0), (272, 0)], [(512, 512), (512, 192)]]
+CHUNK = 128
+CHUNKS = S // CHUNK
+HALF = S // 2
 
 
 def tile_picked_ema_tanh_e_kernel(
@@ -50,20 +48,15 @@ def tile_picked_ema_tanh_e_kernel(
 
         x_rows = xT.rearrange("(z p u e) t -> z u p e t", z=PASSES, p=P, u=2, e=2)
         raw = {}
-
-        def load_half(z, u, h):
-            t = sb.tile([P, 2, HALF], F32, name="raw%d%d%d" % (z, u, h), tag="raw%d%d%d" % (z, u, h), align_bytes=64)
-            nc.sync.dma_start(out=t[:], in_=x_rows[z, u, :, :, h * HALF : (h + 1) * HALF])
-            raw[z, u, h] = t
-
-        load_half(0, 0, 0)
-        nc.sync.dma_start(offs_t[:], offs)
-        load_half(0, 0, 1)
-        load_half(0, 1, 0)
-        load_half(0, 1, 1)
-        for u in range(2):
-            for h in range(2):
-                load_half(1, u, h)
+        for pair in range(4):
+            a = 0
+            for i, (width, scalar_cols) in enumerate(LOADS[pair]):
+                name = "raw%d%d" % (pair, i)
+                raw[pair, i] = sb.tile([P, 2, width], F32, name=name, tag=name, align_bytes=64)
+                nc.sync.dma_start(out=raw[pair, i][:], in_=x_rows[pair // 2, pair % 2, :, :, a : a + width])
+                if (pair, i) == (0, 0):
+                    nc.sync.dma_start(offs_t[:], offs)
+                a = a + width
         nc.sync.dma_start(
             out=w_words[:].bitcast(I32),
             in_=w1_words.rearrange("z p n t -> p z (n t)").bitcast(I32),
@@ -78,28 +71,39 @@ def tile_picked_ema_tanh_e_kernel(
         nc.sync.dma_start(out=old_row[:], in_=old)
         nc.sync.dma_start(out=new_row[:], in_=new)
 
-        def cast(engine_copy, pairs, z, u, h, a, b):
+        def cast(engine_copy, pairs, source, at, a, b):
             engine_copy(
-                pairs[:, 2 * (h * HALF + a) : 2 * (h * HALF + b)].rearrange("p (t e) -> p t e", e=2),
-                raw[z, u, h][:, :, a:b].rearrange("p e t -> p t e"),
+                pairs[:, 2 * (at + a) : 2 * (at + b)].rearrange("p (t e) -> p t e", e=2),
+                source[:, :, a:b].rearrange("p e t -> p t e"),
             )
 
-        def make_pairs(z, u, vector_cols):
-            pairs = sb.tile([P, 2 * T], BF16, name="pairs%d%d" % (z, u), align_bytes=64)
-            cast(nc.scalar.copy, pairs, z, u, 0, 0, HALF)
-            if vector_cols < HALF:
-                cast(nc.scalar.copy, pairs, z, u, 1, vector_cols, HALF)
-            if vector_cols > 0:
-                cast(nc.vector.tensor_copy, pairs, z, u, 1, 0, vector_cols)
+        def make_pairs(pair):
+            pairs = sb.tile([P, 2 * T], BF16, name="pairs%d" % pair, align_bytes=64)
+            at = 0
+            for i, (width, scalar_cols) in enumerate(LOADS[pair]):
+                if scalar_cols > 0:
+                    cast(nc.scalar.copy, pairs, raw[pair, i], at, 0, scalar_cols)
+                if scalar_cols < width:
+                    cast(nc.vector.tensor_copy, pairs, raw[pair, i], at, scalar_cols, width)
+                at = at + width
             return pairs[:].bitcast(U32)
 
-        def quantise(woven, z, a, b, tag):
-            codes = sb.tile([P, b - a], U32, name="codes%d_%d" % (z, a), tag=tag, align_bytes=64)
-            scales = sb.tile([P, b - a], U8, name="scales%d_%d" % (z, a), align_bytes=64)
+        def gather(picked, u, window, a, b):
+            nc.vector.tensor_copy(picked[:, u, :], window.indirect(offs_t[:, a // 16 : b // 16]))
+
+        def weave(engine_copy, picked, name, tag, dtype):
+            woven = sb.tile([P, picked.shape[2], 2], U32, name=name, tag=tag, align_bytes=64)
+            engine_copy(woven[:].bitcast(dtype), picked[:].bitcast(dtype).rearrange("p u j -> p j u"))
+            return woven
+
+        def quantise(woven, name, tag):
+            width = woven.shape[1]
+            codes = sb.tile([P, width], U32, name="codes" + name, tag=tag, align_bytes=64)
+            scales = sb.tile([P, width], U8, name="scales" + name, align_bytes=64)
             nc.vector.quantize_mx(
                 out=codes[:].bitcast(FP8X4),
                 scales=scales[:],
-                in_=woven.rearrange("p j u -> p (j u)").bitcast(BF16),
+                in_=woven[:].rearrange("p j u -> p (j u)").bitcast(BF16),
             )
             return codes, scales
 
@@ -114,59 +118,47 @@ def tile_picked_ema_tanh_e_kernel(
                 stop=(z == PASSES - 1),
             )
 
-        front = FRONT
-        back = BACK
-        accs = [ps.tile([P, b - a], F32, name="acc%d" % a) for a, b in front]
+        accs = [ps.tile([P, CHUNK], F32, name="acc%d" % c) for c in range(CHUNKS)]
 
-        picked0 = sb.tile([P, 2, S], U32, name="picked0")
+        picked0 = [sb.tile([P, 2, HALF], U32, name="picked0_%d" % h) for h in range(2)]
         for u in range(2):
-            window = make_pairs(0, u, VECTOR_COLS[u])
-            nc.vector.tensor_copy(picked0[:, u, :], window.indirect(offs_t[:]))
+            window = make_pairs(u)
+            for h in range(2):
+                gather(picked0[h], u, window, h * HALF, (h + 1) * HALF)
 
-        def first_pass(piece):
-            a0, b0, tag = PASS0[piece]
-            woven = sb.tile([P, b0 - a0, 2], U32, name="woven0_%d" % a0, tag=tag, align_bytes=64)
-            nc.scalar.copy(woven[:], picked0[:, :, a0:b0].rearrange("p u j -> p j u"))
-            codes0, scales0 = quantise(woven[:], 0, a0, b0, "codes0_%d" % a0)
-            for c, (a, b) in enumerate(front):
-                if a0 <= a < b0:
-                    product(accs[c], 0, codes0[:, a - a0 : b - a0], scales0[:, a - a0 : b - a0])
+        def first_pass(h):
+            woven = weave(nc.scalar.copy, picked0[h], "woven0_%d" % h, ["woven0_0", "woven0_1"][h], U32)
+            codes, scales = quantise(woven, "0_%d" % h, ["raw21", "raw30"][h])
+            for c in range(2):
+                cols = slice(c * CHUNK, (c + 1) * CHUNK)
+                product(accs[2 * h + c], 0, codes[:, cols], scales[:, cols])
 
-        picked1 = [sb.tile([P, 2, b - a], U32, name="picked1_%d" % a) for a, b in front]
-        for u in range(2):
-            window = make_pairs(1, u, VECTOR_COLS[2 + u])
-            for c, (a, b) in enumerate(front):
-                nc.vector.tensor_copy(picked1[c][:, u, :], window.indirect(offs_t[:, a // 16 : b // 16]))
-            first_pass(u)
-        woven1 = []
-        for c, (a, b) in enumerate(front):
-            woven = sb.tile([P, b - a, 2], U32, name="woven1_%d" % a, tag="woven1_%d" % a, align_bytes=64)
-            nc.scalar.copy(woven[:], picked1[c][:].rearrange("p u j -> p j u"))
-            woven1.append(woven)
-        for c, (a, b) in enumerate(front):
-            codes, scales = quantise(woven1[c][:], 1, a, b, "codes1_%d" % a)
+        picked1 = [sb.tile([P, 2, CHUNK], U32, name="picked1_%d" % c) for c in range(CHUNKS)]
+        window = make_pairs(2)
+        first_pass(0)
+        for c in range(CHUNKS):
+            gather(picked1[c], 0, window, c * CHUNK, (c + 1) * CHUNK)
+        first_pass(1)
+        window = make_pairs(3)
+        for c in range(CHUNKS):
+            gather(picked1[c], 1, window, c * CHUNK, (c + 1) * CHUNK)
+        y = sb.tile([P, S], F32, name="y")
+
+        def second_pass(c, woven):
+            codes, scales = quantise(woven, "1_%d" % c, "codes1_%d" % c)
             product(accs[c], 1, codes[:], scales[:])
-        ys = [sb.tile([P, b - a], F32, name="y%d" % a) for a, b in back]
-        for c, (a, b) in enumerate(front):
-            g = max(i for i in range(len(back)) if back[i][0] <= a)
-            nc.scalar.activation(ys[g][:, a - back[g][0] : b - back[g][0]], accs[c][:], TANH)
-        moved = [old_row[:, a:b] for a, b in back]
+            nc.scalar.activation(y[:, c * CHUNK : (c + 1) * CHUNK], accs[c][:], TANH)
 
-        def scale_new(g):
-            a, b = back[g]
-            nc.vector.tensor_tensor(moved[g], ys[g][:], new_row[:, a:b], MULT)
+        woven1 = [weave(nc.scalar.copy, picked1[c], "woven1_%d" % c, "woven1_%d" % c, U32) for c in range(CHUNKS - 1)]
+        second_pass(0, woven1[0])
+        second_pass(1, woven1[1])
+        last = weave(nc.vector.tensor_copy, picked1[CHUNKS - 1], "woven1_3", "woven1_0", I32)
+        second_pass(2, woven1[2])
+        second_pass(3, last)
 
-        kept = [sb.tile([P, b - a], F32, name="kept%d" % a, tag=KEPT_TAGS[g], align_bytes=64) for g, (a, b) in enumerate(back)]
-
-        def scale_old(g):
-            a, b = back[g]
-            nc.vector.tensor_tensor(kept[g][:], mem_t[:].indirect(slot_t[:, a // 16 : b // 16]), old_row[:, a:b], MULT)
-
-        def put(g):
-            a, b = back[g]
-            nc.vector.tensor_tensor(mem_t[:].indirect(slot_t[:, a // 16 : b // 16]), moved[g], kept[g][:], ADD)
-
-        for step in (scale_old, scale_new, put):
-            for g in range(len(back)):
-                step(g)
+        kept = sb.tile([P, S], F32, name="kept", tag="woven1_2", align_bytes=64)
+        nc.vector.tensor_tensor(kept[:], mem_t[:].indirect(slot_t[:]), old_row[:], MULT)
+        moved = sb.tile([P, S], F32, name="moved")
+        nc.vector.tensor_tensor(moved[:], y[:], new_row[:], MULT)
+        nc.vector.tensor_tensor(mem_t[:].indirect(slot_t[:]), moved[:], kept[:], ADD)
         nc.sync.dma_start(out=out, in_=mem_t[:])

@@ -43,6 +43,11 @@ def tile_picked_ema_tanh_e_kernel(
         warm_out = sb.tile([P, 1], F32, name="warm_out")
 
         nc.vector.memset(w_scales[:].bitcast(I32), 0)
+        for q in range(4):
+            nc.sync.dma_start(
+                out=w_scales[32 * q : 32 * q + 4, :, :].bitcast(I32),
+                in_=w1_scales[:, 4 * q : 4 * q + 4, :].rearrange("z r n -> r z n").bitcast(I32),
+            )
         nc.vector.memset(warm_in[:], 0.0)
         nc.scalar.activation(warm_out[:], warm_in[:], TANH)
 
@@ -61,13 +66,8 @@ def tile_picked_ema_tanh_e_kernel(
             out=w_words[:].bitcast(I32),
             in_=w1_words.rearrange("z p n t -> p z (n t)").bitcast(I32),
         )
-        for q in range(4):
-            nc.sync.dma_start(
-                out=w_scales[32 * q : 32 * q + 4, :, :].bitcast(I32),
-                in_=w1_scales[:, 4 * q : 4 * q + 4, :].rearrange("z r n -> r z n").bitcast(I32),
-            )
-        nc.sync.dma_start(slot_t[:], slot)
         nc.sync.dma_start(out=mem_t[:], in_=mem)
+        nc.sync.dma_start(slot_t[:], slot)
         nc.sync.dma_start(out=old_row[:], in_=old)
         nc.sync.dma_start(out=new_row[:], in_=new)
 

@@ -18,7 +18,8 @@ TANH = mybir.ActivationFunctionType.Tanh
 
 P = 128
 PASSES = 2
-LOADS = [[(512, 512), (512, 192)], [(512, 512), (512, 192)], [(304, 304), (448, 0), (272, 0)], [(512, 512), (512, 192)]]
+LOADS = [[(512, 512), (512, 192)], [(384, 384), (384, 256), (256, 64)], [(336, 336), (432, 0), (256, 0)], [(384, 384), (384, 256), (256, 64)]]
+SCALE_AFTER = [(0, 1), (1, 0), (2, 0), (2, 1)]
 CHUNK = 128
 CHUNKS = S // CHUNK
 HALF = S // 2
@@ -35,7 +36,8 @@ def tile_picked_ema_tanh_e_kernel(
         offs_t = sb.tile([P, S // 16], U16, name="offs_t")
         slot_t = sb.tile([P, S // 16], U16, name="slot_t")
         mem_t = sb.tile([P, U], F32, name="mem_t")
-        old_row = sb.tile([P, S], F32, name="old_row")
+        old_first = sb.tile([P, CHUNK], F32, name="old_first")
+        old_rest = sb.tile([P, S - CHUNK], F32, name="old_rest")
         new_row = sb.tile([P, S], F32, name="new_row")
         w_words = sb.tile([P, PASSES, N], U32, name="w_words", align_bytes=64)
         w_scales = sb.tile([P, PASSES, N], U8, name="w_scales", align_bytes=64)
@@ -43,13 +45,14 @@ def tile_picked_ema_tanh_e_kernel(
         warm_out = sb.tile([P, 1], F32, name="warm_out")
 
         nc.vector.memset(w_scales[:].bitcast(I32), 0)
-        for q in range(4):
+        nc.vector.memset(warm_in[:], 0.0)
+        nc.scalar.activation(warm_out[:], warm_in[:], TANH)
+
+        def load_scale_rows(q):
             nc.sync.dma_start(
                 out=w_scales[32 * q : 32 * q + 4, :, :].bitcast(I32),
                 in_=w1_scales[:, 4 * q : 4 * q + 4, :].rearrange("z r n -> r z n").bitcast(I32),
             )
-        nc.vector.memset(warm_in[:], 0.0)
-        nc.scalar.activation(warm_out[:], warm_in[:], TANH)
 
         x_rows = xT.rearrange("(z p u e) t -> z u p e t", z=PASSES, p=P, u=2, e=2)
         raw = {}
@@ -57,18 +60,25 @@ def tile_picked_ema_tanh_e_kernel(
             a = 0
             for i, (width, scalar_cols) in enumerate(LOADS[pair]):
                 name = "raw%d%d" % (pair, i)
-                raw[pair, i] = sb.tile([P, 2, width], F32, name=name, tag=name, align_bytes=64)
-                nc.sync.dma_start(out=raw[pair, i][:], in_=x_rows[pair // 2, pair % 2, :, :, a : a + width])
+                if (pair, i) == (2, 0):
+                    shared = sb.tile([P, 2 * S], F32, name=name, tag=name, align_bytes=64)
+                    raw[pair, i] = shared[:, : 2 * width].rearrange("p (e t) -> p e t", e=2)
+                else:
+                    raw[pair, i] = sb.tile([P, 2, width], F32, name=name, tag=name, align_bytes=64)[:]
+                nc.sync.dma_start(out=raw[pair, i], in_=x_rows[pair // 2, pair % 2, :, :, a : a + width])
                 if (pair, i) == (0, 0):
                     nc.sync.dma_start(offs_t[:], offs)
+                if (pair, i) in SCALE_AFTER:
+                    load_scale_rows(SCALE_AFTER.index((pair, i)))
                 a = a + width
+        nc.sync.dma_start(slot_t[:], slot)
+        nc.sync.dma_start(out=mem_t[:], in_=mem)
+        nc.sync.dma_start(out=old_first[:], in_=old[:, :CHUNK])
         nc.sync.dma_start(
             out=w_words[:].bitcast(I32),
             in_=w1_words.rearrange("z p n t -> p z (n t)").bitcast(I32),
         )
-        nc.sync.dma_start(out=mem_t[:], in_=mem)
-        nc.sync.dma_start(slot_t[:], slot)
-        nc.sync.dma_start(out=old_row[:], in_=old)
+        nc.sync.dma_start(out=old_rest[:], in_=old[:, CHUNK:])
         nc.sync.dma_start(out=new_row[:], in_=new)
 
         def cast(engine_copy, pairs, source, at, a, b):
@@ -91,19 +101,18 @@ def tile_picked_ema_tanh_e_kernel(
         def gather(picked, u, window, a, b):
             nc.vector.tensor_copy(picked[:, u, :], window.indirect(offs_t[:, a // 16 : b // 16]))
 
-        def weave(engine_copy, picked, name, tag, dtype):
-            woven = sb.tile([P, picked.shape[2], 2], U32, name=name, tag=tag, align_bytes=64)
-            engine_copy(woven[:].bitcast(dtype), picked[:].bitcast(dtype).rearrange("p u j -> p j u"))
+        def weave(picked, woven):
+            nc.scalar.copy(woven, picked[:, :, :].rearrange("p u j -> p j u"))
             return woven
 
-        def quantise(woven, name, tag):
+        def quantise(woven, name, tag, scale_tag):
             width = woven.shape[1]
             codes = sb.tile([P, width], U32, name="codes" + name, tag=tag, align_bytes=64)
-            scales = sb.tile([P, width], U8, name="scales" + name, align_bytes=64)
+            scales = sb.tile([P, width], U8, name="scales" + name, tag=scale_tag, align_bytes=64)
             nc.vector.quantize_mx(
                 out=codes[:].bitcast(FP8X4),
                 scales=scales[:],
-                in_=woven[:].rearrange("p j u -> p (j u)").bitcast(BF16),
+                in_=woven.rearrange("p j u -> p (j u)").bitcast(BF16),
             )
             return codes, scales
 
@@ -127,38 +136,44 @@ def tile_picked_ema_tanh_e_kernel(
                 gather(picked0[h], u, window, h * HALF, (h + 1) * HALF)
 
         def first_pass(h):
-            woven = weave(nc.scalar.copy, picked0[h], "woven0_%d" % h, ["woven0_0", "woven0_1"][h], U32)
-            codes, scales = quantise(woven, "0_%d" % h, ["raw21", "raw30"][h])
+            woven = weave(picked0[h], shared[:, h * S : (h + 1) * S].bitcast(U32).rearrange("p (j u) -> p j u", u=2))
+            codes, scales = quantise(woven, "0_%d" % h, ["raw21", "raw31"][h], "scales0_%d" % h)
             for c in range(2):
                 cols = slice(c * CHUNK, (c + 1) * CHUNK)
                 product(accs[2 * h + c], 0, codes[:, cols], scales[:, cols])
 
-        picked1 = [sb.tile([P, 2, CHUNK], U32, name="picked1_%d" % c) for c in range(CHUNKS)]
+        both1 = sb.tile([P, 2, S], U32, name="both1", align_bytes=64)
+        picked1 = [both1[:, :, c * CHUNK : (c + 1) * CHUNK] for c in range(CHUNKS)]
+        kept_t = sb.tile([P, S], F32, name="kept_t")
+        kept = kept_t[:]
         window = make_pairs(2)
         first_pass(0)
-        for c in range(CHUNKS):
-            gather(picked1[c], 0, window, c * CHUNK, (c + 1) * CHUNK)
-        first_pass(1)
+        gather(both1, 0, window, 0, S)
         window = make_pairs(3)
+        first_pass(1)
         for c in range(CHUNKS):
             gather(picked1[c], 1, window, c * CHUNK, (c + 1) * CHUNK)
         y = sb.tile([P, S], F32, name="y")
 
         def second_pass(c, woven):
-            codes, scales = quantise(woven, "1_%d" % c, "codes1_%d" % c)
+            codes, scales = quantise(woven, "1_%d" % c, ["codes1_0", "codes1_1", "raw21", "codes1_3"][c], ["scales1_0", "scales1_1", "scales1_2", "scales0_0"][c])
             product(accs[c], 1, codes[:], scales[:])
             nc.scalar.activation(y[:, c * CHUNK : (c + 1) * CHUNK], accs[c][:], TANH)
 
-        woven1 = [weave(nc.scalar.copy, picked1[c], "woven1_%d" % c, "woven1_%d" % c, U32) for c in range(CHUNKS - 1)]
+        def look_up(a, b, old_part):
+            nc.vector.tensor_tensor(kept[:, a:b], mem_t[:].indirect(slot_t[:, a // 16 : b // 16]), old_part[:], MULT)
+
+        woven1 = [
+            weave(picked1[c], sb.tile([P, CHUNK, 2], U32, name="woven1_%d" % c, align_bytes=64)[:]) for c in range(CHUNKS)
+        ]
         second_pass(0, woven1[0])
         second_pass(1, woven1[1])
-        last = weave(nc.vector.tensor_copy, picked1[CHUNKS - 1], "woven1_3", "woven1_0", I32)
+        look_up(0, CHUNK, old_first)
         second_pass(2, woven1[2])
-        second_pass(3, last)
-
-        kept = sb.tile([P, S], F32, name="kept", tag="woven1_2", align_bytes=64)
-        nc.vector.tensor_tensor(kept[:], mem_t[:].indirect(slot_t[:]), old_row[:], MULT)
+        second_pass(3, woven1[3])
+        look_up(CHUNK, S, old_rest)
         moved = sb.tile([P, S], F32, name="moved")
-        nc.vector.tensor_tensor(moved[:], y[:], new_row[:], MULT)
-        nc.vector.tensor_tensor(mem_t[:].indirect(slot_t[:]), moved[:], kept[:], ADD)
+        for a, b in ((0, S - CHUNK), (S - CHUNK, S)):
+            nc.vector.tensor_tensor(moved[:, a:b], y[:, a:b], new_row[:, a:b], MULT)
+        nc.vector.tensor_tensor(mem_t[:].indirect(slot_t[:]), moved[:], kept, ADD)
         nc.sync.dma_start(out=out, in_=mem_t[:])

@@ -19,7 +19,7 @@ TANH = mybir.ActivationFunctionType.Tanh
 P = 128
 PASSES = 2
 LOADS = [[(512, 512), (512, 192)], [(384, 384), (384, 256), (256, 64)], [(336, 336), (432, 0), (256, 0)], [(384, 384), (384, 256), (256, 64)]]
-SCALE_AFTER = [(0, 1), (1, 0), (2, 0), (2, 1)]
+SCALE_AFTER = [(0, 1), (1, 0), (1, 1), (1, 2)]
 CHUNK = 128
 CHUNKS = S // CHUNK
 HALF = S // 2

@@ -15,14 +15,14 @@ FP8X4 = mybir.dt.float8_e4m3fn_x4
 MULT = mybir.AluOpType.mult
 ADD = mybir.AluOpType.add
 TANH = mybir.ActivationFunctionType.Tanh
+COPY = mybir.ActivationFunctionType.Copy
 
 P = 128
 PASSES = 2
-LOADS = [[(512, 512), (512, 192)], [(384, 384), (384, 256), (256, 64)], [(336, 336), (432, 0), (256, 0)], [(384, 384), (384, 256), (256, 64)]]
-SCALE_AFTER = [(0, 1), (1, 0), (1, 1), (1, 2)]
+PACK = 4
 CHUNK = 128
-CHUNKS = S // CHUNK
 HALF = S // 2
+PARTS = [(0, CHUNK), (CHUNK, HALF), (HALF, S)]
 
 
 def tile_picked_ema_tanh_e_kernel(
@@ -36,10 +36,8 @@ def tile_picked_ema_tanh_e_kernel(
         offs_t = sb.tile([P, S // 16], U16, name="offs_t")
         slot_t = sb.tile([P, S // 16], U16, name="slot_t")
         mem_t = sb.tile([P, U], F32, name="mem_t")
-        old_first = sb.tile([P, CHUNK], F32, name="old_first")
-        old_rest = sb.tile([P, S - CHUNK], F32, name="old_rest")
-        new_row = sb.tile([P, S], F32, name="new_row")
-        w_words = sb.tile([P, PASSES, N], U32, name="w_words", align_bytes=64)
+        shares = [sb.tile([P, 2, HALF], F32, name="shares%d" % h) for h in range(2)]
+        w_words = [sb.tile([P, N], U32, name="w_words%d" % z, align_bytes=64) for z in range(PASSES)]
         w_scales = sb.tile([P, PASSES, N], U8, name="w_scales", align_bytes=64)
         warm_in = sb.tile([P, 1], F32, name="warm_in")
         warm_out = sb.tile([P, 1], F32, name="warm_out")
@@ -54,72 +52,63 @@ def tile_picked_ema_tanh_e_kernel(
                 in_=w1_scales[:, 4 * q : 4 * q + 4, :].rearrange("z r n -> r z n").bitcast(I32),
             )
 
-        x_rows = xT.rearrange("(z p u e) t -> z u p e t", z=PASSES, p=P, u=2, e=2)
-        raw = {}
-        for pair in range(4):
-            a = 0
-            for i, (width, scalar_cols) in enumerate(LOADS[pair]):
-                name = "raw%d%d" % (pair, i)
-                if (pair, i) == (2, 0):
-                    shared = sb.tile([P, 2 * S], F32, name=name, tag=name, align_bytes=64)
-                    raw[pair, i] = shared[:, : 2 * width].rearrange("p (e t) -> p e t", e=2)
-                else:
-                    raw[pair, i] = sb.tile([P, 2, width], F32, name=name, tag=name, align_bytes=64)[:]
-                nc.sync.dma_start(out=raw[pair, i], in_=x_rows[pair // 2, pair % 2, :, :, a : a + width])
-                if (pair, i) == (0, 0):
-                    nc.sync.dma_start(offs_t[:], offs)
-                if (pair, i) in SCALE_AFTER:
-                    load_scale_rows(SCALE_AFTER.index((pair, i)))
-                a = a + width
-        nc.sync.dma_start(slot_t[:], slot)
-        nc.sync.dma_start(out=mem_t[:], in_=mem)
-        nc.sync.dma_start(out=old_first[:], in_=old[:, :CHUNK])
-        nc.sync.dma_start(
-            out=w_words[:].bitcast(I32),
-            in_=w1_words.rearrange("z p n t -> p z (n t)").bitcast(I32),
-        )
-        nc.sync.dma_start(out=old_rest[:], in_=old[:, CHUNK:])
-        nc.sync.dma_start(out=new_row[:], in_=new)
-
-        def cast(engine_copy, pairs, source, at, a, b):
-            engine_copy(
-                pairs[:, 2 * (at + a) : 2 * (at + b)].rearrange("p (t e) -> p t e", e=2),
-                source[:, :, a:b].rearrange("p e t -> p t e"),
+        def load_weights(z):
+            nc.sync.dma_start(
+                out=w_words[z][:].bitcast(I32),
+                in_=w1_words[z].rearrange("p n t -> p (n t)").bitcast(I32),
             )
 
-        def make_pairs(pair):
-            pairs = sb.tile([P, 2 * T], BF16, name="pairs%d" % pair, align_bytes=64)
-            at = 0
-            for i, (width, scalar_cols) in enumerate(LOADS[pair]):
-                if scalar_cols > 0:
-                    cast(nc.scalar.copy, pairs, raw[pair, i], at, 0, scalar_cols)
-                if scalar_cols < width:
-                    cast(nc.vector.tensor_copy, pairs, raw[pair, i], at, scalar_cols, width)
-                at = at + width
-            return pairs[:].bitcast(U32)
+        x_rows = xT.rearrange("(z p t) c -> z t p c", z=PASSES, p=P, t=PACK)
+        rows = [sb.tile([P, T], F32, name="row%d" % r) for r in range(PASSES * PACK)]
+        nc.sync.dma_start(offs_t[:], offs)
+        for r in range(PASSES * PACK):
+            nc.sync.dma_start(out=rows[r][:], in_=x_rows[r // PACK, r % PACK])
+            if r < 4:
+                load_scale_rows(r)
+            if r == 4:
+                nc.sync.dma_start(slot_t[:], slot)
+        load_weights(0)
+        nc.sync.dma_start(out=mem_t[:], in_=mem)
+        load_weights(1)
+        for h in range(2):
+            for i, share in enumerate((old, new)):
+                nc.sync.dma_start(out=shares[h][:, i, :], in_=share[:, h * HALF : (h + 1) * HALF])
 
-        def gather(picked, u, window, a, b):
-            nc.vector.tensor_copy(picked[:, u, :], window.indirect(offs_t[:, a // 16 : b // 16]))
+        picked = [sb.tile([P, PACK, S], BF16, name="picked%d" % z, align_bytes=64) for z in range(PASSES)]
+        first_woven = sb.tile([P, CHUNK, PACK], BF16, name="first_woven", align_bytes=64)
 
-        def weave(picked, woven):
-            nc.scalar.copy(woven, picked[:, :, :].rearrange("p u j -> p j u"))
+        def entries(listed, a, b):
+            return listed[:, a // 16 : b // 16]
+
+        def pick_scalar(r, a, b):
+            nc.scalar.activation(picked[r // PACK][:, r % PACK, a:b], rows[r][:].indirect(entries(offs_t, a, b)), COPY)
+
+        def pick_vector(r, a, b):
+            nc.vector.tensor_copy(picked[r // PACK][:, r % PACK, a:b], rows[r][:].indirect(entries(offs_t, a, b)))
+
+        def pick_woven(r):
+            nc.vector.tensor_copy(first_woven[:, :, r % PACK], rows[r][:].indirect(entries(offs_t, 0, CHUNK)))
+
+        def weave(z, a, b):
+            woven = sb.tile([P, b - a, PACK], BF16, name="woven%d_%d" % (z, a), align_bytes=64)
+            nc.vector.tensor_copy(woven[:], picked[z][:, :, a:b].rearrange("p t j -> p j t"))
             return woven
 
-        def quantise(woven, name, tag, scale_tag):
+        def quantise(woven, name, tag):
             width = woven.shape[1]
             codes = sb.tile([P, width], U32, name="codes" + name, tag=tag, align_bytes=64)
-            scales = sb.tile([P, width], U8, name="scales" + name, tag=scale_tag, align_bytes=64)
+            scales = sb.tile([P, width], U8, name="scales" + name, align_bytes=64)
             nc.vector.quantize_mx(
                 out=codes[:].bitcast(FP8X4),
                 scales=scales[:],
-                in_=woven.rearrange("p j u -> p (j u)").bitcast(BF16),
+                in_=woven[:].rearrange("p j t -> p (j t)"),
             )
             return codes, scales
 
         def product(acc, z, codes, scales):
             nc.tensor.matmul_mx(
                 out=acc[:],
-                lhsT=w_words[:, z, :].bitcast(FP8X4),
+                lhsT=w_words[z][:].bitcast(FP8X4),
                 lhsT_scale=w_scales[:, z, :],
                 rhs=codes.bitcast(FP8X4),
                 rhs_scale=scales,
@@ -127,53 +116,72 @@ def tile_picked_ema_tanh_e_kernel(
                 stop=(z == PASSES - 1),
             )
 
-        accs = [ps.tile([P, CHUNK], F32, name="acc%d" % c) for c in range(CHUNKS)]
+        accs = [ps.tile([P, b - a], F32, name="acc%d" % a) for a, b in PARTS]
 
-        picked0 = [sb.tile([P, 2, HALF], U32, name="picked0_%d" % h) for h in range(2)]
-        for u in range(2):
-            window = make_pairs(u)
-            for h in range(2):
-                gather(picked0[h], u, window, h * HALF, (h + 1) * HALF)
+        pick_scalar(0, 0, S)
+        pick_vector(1, 0, S)
+        pick_scalar(2, 0, S)
+        pick_scalar(3, 0, HALF)
+        pick_vector(3, HALF, S)
+        halves = [weave(0, 0, HALF), weave(0, HALF, S)]
+        codes, scales = quantise(halves[0], "0_0", "codes0_0")
+        for c, (a, b) in enumerate(PARTS[:2]):
+            product(accs[c], 0, codes[:, a:b], scales[:, a:b])
+        pick_scalar(4, CHUNK, S)
+        pick_woven(4)
+        codes, scales = quantise(halves[1], "0_1", "codes0_1")
+        product(accs[2], 0, codes[:], scales[:])
+        for r in (5, 6):
+            pick_scalar(r, CHUNK, S)
+            pick_woven(r)
+        pick_woven(7)
+        for a, b in PARTS[1:]:
+            pick_scalar(7, a, b)
 
-        def first_pass(h):
-            woven = weave(picked0[h], shared[:, h * S : (h + 1) * S].bitcast(U32).rearrange("p (j u) -> p j u", u=2))
-            codes, scales = quantise(woven, "0_%d" % h, ["raw21", "raw31"][h], "scales0_%d" % h)
-            for c in range(2):
-                cols = slice(c * CHUNK, (c + 1) * CHUNK)
-                product(accs[2 * h + c], 0, codes[:, cols], scales[:, cols])
+        def look_up(c, tag):
+            a, b = PARTS[c]
+            terms = sb.tile([P, 2, b - a], F32, name="terms%d" % c, tag=tag, align_bytes=64)
+            nc.scalar.activation(terms[:, 0, :], mem_t[:].indirect(entries(slot_t, a, b)), COPY)
+            return terms
 
-        both1 = sb.tile([P, 2, S], U32, name="both1", align_bytes=64)
-        picked1 = [both1[:, :, c * CHUNK : (c + 1) * CHUNK] for c in range(CHUNKS)]
-        kept_t = sb.tile([P, S], F32, name="kept_t")
-        kept = kept_t[:]
-        window = make_pairs(2)
-        first_pass(0)
-        gather(both1, 0, window, 0, S)
-        window = make_pairs(3)
-        first_pass(1)
-        for c in range(CHUNKS):
-            gather(picked1[c], 1, window, c * CHUNK, (c + 1) * CHUNK)
-        y = sb.tile([P, S], F32, name="y")
-
-        def second_pass(c, woven):
-            codes, scales = quantise(woven, "1_%d" % c, ["codes1_0", "codes1_1", "raw21", "codes1_3"][c], ["scales1_0", "scales1_1", "scales1_2", "scales0_0"][c])
+        def second_pass(c, woven, tag):
+            codes, scales = quantise(woven, "1_%d" % c, tag)
             product(accs[c], 1, codes[:], scales[:])
-            nc.scalar.activation(y[:, c * CHUNK : (c + 1) * CHUNK], accs[c][:], TANH)
 
-        def look_up(a, b, old_part):
-            nc.vector.tensor_tensor(kept[:, a:b], mem_t[:].indirect(slot_t[:, a // 16 : b // 16]), old_part[:], MULT)
+        def squash(c, terms):
+            nc.scalar.activation(terms[:, 1, :], accs[c][:], TANH)
 
-        woven1 = [
-            weave(picked1[c], sb.tile([P, CHUNK, 2], U32, name="woven1_%d" % c, align_bytes=64)[:]) for c in range(CHUNKS)
-        ]
-        second_pass(0, woven1[0])
-        second_pass(1, woven1[1])
-        look_up(0, CHUNK, old_first)
-        second_pass(2, woven1[2])
-        second_pass(3, woven1[3])
-        look_up(CHUNK, S, old_rest)
-        moved = sb.tile([P, S], F32, name="moved")
-        for a, b in ((0, S - CHUNK), (S - CHUNK, S)):
-            nc.vector.tensor_tensor(moved[:, a:b], y[:, a:b], new_row[:, a:b], MULT)
-        nc.vector.tensor_tensor(mem_t[:].indirect(slot_t[:]), moved[:], kept, ADD)
+        def scale(c, terms, tag):
+            a, b = PARTS[c]
+            scaled = sb.tile([P, 2, b - a], F32, name="scaled%d" % c, tag=tag)
+            nc.vector.tensor_tensor(scaled[:], terms[:], shares[a // HALF][:, :, a % HALF : a % HALF + b - a], MULT)
+            return scaled
+
+        def add(c, scaled, tag):
+            total = sb.tile([P, CHUNK], F32, name="total%d" % c, tag=tag, align_bytes=64)
+            nc.vector.tensor_tensor(total[:], scaled[:, 0, :], scaled[:, 1, :], ADD)
+            return total
+
+        def put(c, total):
+            nc.scalar.activation(mem_t[:].indirect(entries(slot_t, *PARTS[c])), total[:], COPY)
+
+        woven1 = weave(1, *PARTS[1])
+        second_pass(0, first_woven, "ring0")
+        second_pass(1, woven1, "codes1_1")
+        woven2 = weave(1, *PARTS[2])
+        terms0 = look_up(0, "ring2")
+        terms1 = look_up(1, "terms1")
+        squash(0, terms0)
+        terms2 = look_up(2, "ring0")
+        squash(1, terms1)
+        scaled0 = scale(0, terms0, "scaled0")
+        total0 = add(0, scaled0, "total0")
+        put(0, total0)
+        second_pass(2, woven2, "ring2")
+        scaled1 = scale(1, terms1, "scaled0")
+        squash(2, terms2)
+        total1 = add(1, scaled1, "ring2")
+        put(1, total1)
+        scaled2 = scale(2, terms2, "scaled2")
+        nc.vector.tensor_tensor(mem_t[:].indirect(entries(slot_t, *PARTS[2])), scaled2[:, 0, :], scaled2[:, 1, :], ADD)
         nc.sync.dma_start(out=out, in_=mem_t[:])

@@ -39,12 +39,8 @@ def tile_picked_ema_tanh_e_kernel(
         shares = [sb.tile([P, 2, HALF], F32, name="shares%d" % h) for h in range(2)]
         w_words = [sb.tile([P, N], U32, name="w_words%d" % z, align_bytes=64) for z in range(PASSES)]
         w_scales = sb.tile([P, PASSES, N], U8, name="w_scales", align_bytes=64)
-        warm_in = sb.tile([P, 1], F32, name="warm_in")
-        warm_out = sb.tile([P, 1], F32, name="warm_out")
 
         nc.vector.memset(w_scales[:].bitcast(I32), 0)
-        nc.vector.memset(warm_in[:], 0.0)
-        nc.scalar.activation(warm_out[:], warm_in[:], TANH)
 
         def load_scale_rows(q):
             nc.sync.dma_start(

@@ -36,7 +36,8 @@ def tile_picked_ema_tanh_e_kernel(
         offs_t = sb.tile([P, S // 16], U16, name="offs_t")
         slot_t = sb.tile([P, S // 16], U16, name="slot_t")
         mem_t = sb.tile([P, U], F32, name="mem_t")
-        shares = [sb.tile([P, 2, HALF], F32, name="shares%d" % h) for h in range(2)]
+        first_shares = sb.tile([P, 2, CHUNK], F32, name="first_shares")
+        later_shares = sb.tile([P, 2, S - CHUNK], F32, name="later_shares")
         w_words = [sb.tile([P, N], U32, name="w_words%d" % z, align_bytes=64) for z in range(PASSES)]
         w_scales = sb.tile([P, PASSES, N], U8, name="w_scales", align_bytes=64)
 
@@ -56,19 +57,20 @@ def tile_picked_ema_tanh_e_kernel(
 
         x_rows = xT.rearrange("(z p t) c -> z t p c", z=PASSES, p=P, t=PACK)
         rows = [sb.tile([P, T], F32, name="row%d" % r) for r in range(PASSES * PACK)]
-        nc.sync.dma_start(offs_t[:], offs)
         for r in range(PASSES * PACK):
             nc.sync.dma_start(out=rows[r][:], in_=x_rows[r // PACK, r % PACK])
-            if r < 4:
-                load_scale_rows(r)
-            if r == 4:
+            if r == 0:
+                nc.sync.dma_start(offs_t[:], offs)
+            if 1 <= r < 5:
+                load_scale_rows(r - 1)
+            if r == 5:
                 nc.sync.dma_start(slot_t[:], slot)
         load_weights(0)
         nc.sync.dma_start(out=mem_t[:], in_=mem)
         load_weights(1)
-        for h in range(2):
+        for shares, a, b in ((first_shares, 0, CHUNK), (later_shares, CHUNK, S)):
             for i, share in enumerate((old, new)):
-                nc.sync.dma_start(out=shares[h][:, i, :], in_=share[:, h * HALF : (h + 1) * HALF])
+                nc.sync.dma_start(out=shares[:, i, :], in_=share[:, a:b])
 
         picked = [sb.tile([P, PACK, S], BF16, name="picked%d" % z, align_bytes=64) for z in range(PASSES)]
         first_woven = sb.tile([P, CHUNK, PACK], BF16, name="first_woven", align_bytes=64)
@@ -121,12 +123,11 @@ def tile_picked_ema_tanh_e_kernel(
         pick_vector(3, HALF, S)
         halves = [weave(0, 0, HALF), weave(0, HALF, S)]
         codes, scales = quantise(halves[0], "0_0", "codes0_0")
-        for c, (a, b) in enumerate(PARTS[:2]):
-            product(accs[c], 0, codes[:, a:b], scales[:, a:b])
+        first_pass = [(codes[:, a:b], scales[:, a:b]) for a, b in PARTS[:2]]
         pick_scalar(4, CHUNK, S)
         pick_woven(4)
         codes, scales = quantise(halves[1], "0_1", "codes0_1")
-        product(accs[2], 0, codes[:], scales[:])
+        first_pass.append((codes[:], scales[:]))
         for r in (5, 6):
             pick_scalar(r, CHUNK, S)
             pick_woven(r)
@@ -134,50 +135,37 @@ def tile_picked_ema_tanh_e_kernel(
         for a, b in PARTS[1:]:
             pick_scalar(7, a, b)
 
-        def look_up(c, tag):
-            a, b = PARTS[c]
-            terms = sb.tile([P, 2, b - a], F32, name="terms%d" % c, tag=tag, align_bytes=64)
+        def look_up(name, a, b, tag):
+            terms = sb.tile([P, 2, b - a], F32, name=name, tag=tag, align_bytes=64)
             nc.scalar.activation(terms[:, 0, :], mem_t[:].indirect(entries(slot_t, a, b)), COPY)
             return terms
 
         def second_pass(c, woven, tag):
             codes, scales = quantise(woven, "1_%d" % c, tag)
+            product(accs[c], 0, *first_pass[c])
             product(accs[c], 1, codes[:], scales[:])
 
-        def squash(c, terms):
-            nc.scalar.activation(terms[:, 1, :], accs[c][:], TANH)
-
-        def scale(c, terms, tag):
-            a, b = PARTS[c]
-            scaled = sb.tile([P, 2, b - a], F32, name="scaled%d" % c, tag=tag)
-            nc.vector.tensor_tensor(scaled[:], terms[:], shares[a // HALF][:, :, a % HALF : a % HALF + b - a], MULT)
-            return scaled
-
-        def add(c, scaled, tag):
-            total = sb.tile([P, CHUNK], F32, name="total%d" % c, tag=tag, align_bytes=64)
-            nc.vector.tensor_tensor(total[:], scaled[:, 0, :], scaled[:, 1, :], ADD)
-            return total
-
-        def put(c, total):
-            nc.scalar.activation(mem_t[:].indirect(entries(slot_t, *PARTS[c])), total[:], COPY)
-
         woven1 = weave(1, *PARTS[1])
-        second_pass(0, first_woven, "ring0")
+        second_pass(0, first_woven, "ring")
         second_pass(1, woven1, "codes1_1")
         woven2 = weave(1, *PARTS[2])
-        terms0 = look_up(0, "ring2")
-        terms1 = look_up(1, "terms1")
-        squash(0, terms0)
-        terms2 = look_up(2, "ring0")
-        squash(1, terms1)
-        scaled0 = scale(0, terms0, "scaled0")
-        total0 = add(0, scaled0, "total0")
-        put(0, total0)
-        second_pass(2, woven2, "ring2")
-        scaled1 = scale(1, terms1, "scaled0")
-        squash(2, terms2)
-        total1 = add(1, scaled1, "ring2")
-        put(1, total1)
-        scaled2 = scale(2, terms2, "scaled2")
-        nc.vector.tensor_tensor(mem_t[:].indirect(entries(slot_t, *PARTS[2])), scaled2[:, 0, :], scaled2[:, 1, :], ADD)
+        second_pass(2, woven2, "codes1_2")
+        first_terms = look_up("first_terms", 0, CHUNK, "first_terms")
+        nc.scalar.activation(first_terms[:, 1, :], accs[0][:], TANH)
+        later_terms = look_up("later_terms", CHUNK, S, "ring")
+        for c in (1, 2):
+            a, b = PARTS[c]
+            nc.scalar.activation(later_terms[:, 1, a - CHUNK : b - CHUNK], accs[c][:], TANH)
+        first_scaled = sb.tile([P, 2, CHUNK], F32, name="first_scaled")
+        nc.vector.tensor_tensor(first_scaled[:], first_terms[:], first_shares[:], MULT)
+        first_total = sb.tile([P, CHUNK], F32, name="first_total")
+        nc.vector.tensor_tensor(first_total[:], first_scaled[:, 0, :], first_scaled[:, 1, :], ADD)
+        nc.scalar.activation(mem_t[:].indirect(entries(slot_t, 0, CHUNK)), first_total[:], COPY)
+        later_scaled = sb.tile([P, 2, S - CHUNK], F32, name="later_scaled")
+        for a, b in PARTS[1:]:
+            cols = slice(a - CHUNK, b - CHUNK)
+            nc.vector.tensor_tensor(later_scaled[:, :, cols], later_terms[:, :, cols], later_shares[:, :, cols], MULT)
+        nc.vector.tensor_tensor(
+            mem_t[:].indirect(entries(slot_t, CHUNK, S)), later_scaled[:, 0, :], later_scaled[:, 1, :], ADD
+        )
         nc.sync.dma_start(out=out, in_=mem_t[:])

@@ -36,8 +36,8 @@ def tile_picked_ema_tanh_e_kernel(
         offs_t = sb.tile([P, S // 16], U16, name="offs_t")
         slot_t = sb.tile([P, S // 16], U16, name="slot_t")
         mem_t = sb.tile([P, U], F32, name="mem_t")
-        first_shares = sb.tile([P, 2, CHUNK], F32, name="first_shares")
-        later_shares = sb.tile([P, 2, S - CHUNK], F32, name="later_shares")
+        first_shares = sb.tile([P, 3, CHUNK], F32, name="first_shares")
+        later_shares = sb.tile([P, HALF + S - CHUNK], F32, name="later_shares")
         w_words = [sb.tile([P, N], U32, name="w_words%d" % z, align_bytes=64) for z in range(PASSES)]
         w_scales = sb.tile([P, PASSES, N], U8, name="w_scales", align_bytes=64)
 
@@ -68,12 +68,13 @@ def tile_picked_ema_tanh_e_kernel(
         load_weights(0)
         nc.sync.dma_start(out=mem_t[:], in_=mem)
         load_weights(1)
-        for shares, a, b in ((first_shares, 0, CHUNK), (later_shares, CHUNK, S)):
-            for i, share in enumerate((old, new)):
-                nc.sync.dma_start(out=shares[:, i, :], in_=share[:, a:b])
+        nc.sync.dma_start(out=first_shares[:, 0, :], in_=new[:, :CHUNK])
+        nc.sync.dma_start(out=first_shares[:, 1:, :].rearrange("p i j -> p (i j)"), in_=old[:, :HALF])
+        nc.sync.dma_start(out=later_shares[:, :HALF], in_=old[:, HALF:])
+        nc.sync.dma_start(out=later_shares[:, HALF:], in_=new[:, CHUNK:])
 
         picked = [sb.tile([P, PACK, S], BF16, name="picked%d" % z, align_bytes=64) for z in range(PASSES)]
-        first_woven = sb.tile([P, CHUNK, PACK], BF16, name="first_woven", align_bytes=64)
+        first_woven = sb.tile([P, HALF, PACK], BF16, name="first_woven", align_bytes=64)
 
         def entries(listed, a, b):
             return listed[:, a // 16 : b // 16]
@@ -84,13 +85,13 @@ def tile_picked_ema_tanh_e_kernel(
         def pick_vector(r, a, b):
             nc.vector.tensor_copy(picked[r // PACK][:, r % PACK, a:b], rows[r][:].indirect(entries(offs_t, a, b)))
 
-        def pick_woven(r):
-            nc.vector.tensor_copy(first_woven[:, :, r % PACK], rows[r][:].indirect(entries(offs_t, 0, CHUNK)))
+        def pick_woven(r, a, b):
+            nc.vector.tensor_copy(first_woven[:, a:b, r % PACK], rows[r][:].indirect(entries(offs_t, a, b)))
 
         def weave(z, a, b):
             woven = sb.tile([P, b - a, PACK], BF16, name="woven%d_%d" % (z, a), align_bytes=64)
             nc.vector.tensor_copy(woven[:], picked[z][:, :, a:b].rearrange("p t j -> p j t"))
-            return woven
+            return woven[:]
 
         def quantise(woven, name, tag):
             width = woven.shape[1]
@@ -99,7 +100,7 @@ def tile_picked_ema_tanh_e_kernel(
             nc.vector.quantize_mx(
                 out=codes[:].bitcast(FP8X4),
                 scales=scales[:],
-                in_=woven[:].rearrange("p j t -> p (j t)"),
+                in_=woven.rearrange("p j t -> p (j t)"),
             )
             return codes, scales
 
@@ -118,54 +119,52 @@ def tile_picked_ema_tanh_e_kernel(
 
         pick_scalar(0, 0, S)
         pick_vector(1, 0, S)
-        pick_scalar(2, 0, S)
-        pick_scalar(3, 0, HALF)
-        pick_vector(3, HALF, S)
+        for r in (2, 3):
+            pick_scalar(r, 0, HALF)
+            pick_vector(r, HALF, S)
         halves = [weave(0, 0, HALF), weave(0, HALF, S)]
         codes, scales = quantise(halves[0], "0_0", "codes0_0")
         first_pass = [(codes[:, a:b], scales[:, a:b]) for a, b in PARTS[:2]]
-        pick_scalar(4, CHUNK, S)
-        pick_woven(4)
         codes, scales = quantise(halves[1], "0_1", "codes0_1")
         first_pass.append((codes[:], scales[:]))
-        for r in (5, 6):
-            pick_scalar(r, CHUNK, S)
-            pick_woven(r)
-        pick_woven(7)
-        for a, b in PARTS[1:]:
-            pick_scalar(7, a, b)
-
-        def look_up(name, a, b, tag):
-            terms = sb.tile([P, 2, b - a], F32, name=name, tag=tag, align_bytes=64)
-            nc.scalar.activation(terms[:, 0, :], mem_t[:].indirect(entries(slot_t, a, b)), COPY)
-            return terms
+        pick_scalar(4, 0, S)
+        pick_scalar(5, 0, HALF)
+        pick_scalar(5, HALF, S)
+        nc.vector.tensor_copy(first_woven[:, :, :2], picked[1][:, :2, :HALF].rearrange("p t j -> p j t"))
+        pick_scalar(6, HALF, S)
+        pick_woven(6, 0, HALF)
+        pick_scalar(7, HALF, S)
+        for a, b in PARTS[:2]:
+            pick_woven(7, a, b)
 
         def second_pass(c, woven, tag):
             codes, scales = quantise(woven, "1_%d" % c, tag)
             product(accs[c], 0, *first_pass[c])
             product(accs[c], 1, codes[:], scales[:])
 
-        woven1 = weave(1, *PARTS[1])
-        second_pass(0, first_woven, "ring")
-        second_pass(1, woven1, "codes1_1")
+        second_pass(0, first_woven[:, :CHUNK, :], "ring")
         woven2 = weave(1, *PARTS[2])
+        second_pass(1, first_woven[:, CHUNK:, :], "codes1_1")
         second_pass(2, woven2, "codes1_2")
-        first_terms = look_up("first_terms", 0, CHUNK, "first_terms")
-        nc.scalar.activation(first_terms[:, 1, :], accs[0][:], TANH)
-        later_terms = look_up("later_terms", CHUNK, S, "ring")
-        for c in (1, 2):
-            a, b = PARTS[c]
-            nc.scalar.activation(later_terms[:, 1, a - CHUNK : b - CHUNK], accs[c][:], TANH)
+        first_terms = sb.tile([P, 2, CHUNK], F32, name="first_terms")
+        nc.scalar.activation(first_terms[:, 1, :], mem_t[:].indirect(entries(slot_t, 0, CHUNK)), COPY)
+        nc.scalar.activation(first_terms[:, 0, :], accs[0][:], TANH)
+        later_terms = sb.tile([P, HALF + S - CHUNK], F32, name="later_terms", tag="ring", align_bytes=64)
+        nc.scalar.activation(later_terms[:, :HALF], mem_t[:].indirect(entries(slot_t, HALF, S)), COPY)
+        nc.scalar.activation(later_terms[:, HALF : HALF + CHUNK], accs[1][:], TANH)
+        nc.scalar.activation(later_terms[:, HALF + CHUNK :], accs[2][:], TANH)
         first_scaled = sb.tile([P, 2, CHUNK], F32, name="first_scaled")
-        nc.vector.tensor_tensor(first_scaled[:], first_terms[:], first_shares[:], MULT)
+        nc.vector.tensor_tensor(first_scaled[:], first_terms[:], first_shares[:, :2, :], MULT)
+        later_scaled = sb.tile([P, 2 * (S - CHUNK)], F32, name="later_scaled")
+        nc.vector.tensor_tensor(
+            later_scaled[:, :CHUNK], mem_t[:].indirect(entries(slot_t, CHUNK, HALF)), first_shares[:, 2, :], MULT
+        )
         first_total = sb.tile([P, CHUNK], F32, name="first_total")
         nc.vector.tensor_tensor(first_total[:], first_scaled[:, 0, :], first_scaled[:, 1, :], ADD)
         nc.scalar.activation(mem_t[:].indirect(entries(slot_t, 0, CHUNK)), first_total[:], COPY)
-        later_scaled = sb.tile([P, 2, S - CHUNK], F32, name="later_scaled")
-        for a, b in PARTS[1:]:
-            cols = slice(a - CHUNK, b - CHUNK)
-            nc.vector.tensor_tensor(later_scaled[:, :, cols], later_terms[:, :, cols], later_shares[:, :, cols], MULT)
+        for a, b in ((0, HALF + CHUNK), (HALF + CHUNK, HALF + S - CHUNK)):
+            nc.vector.tensor_tensor(later_scaled[:, CHUNK + a : CHUNK + b], later_terms[:, a:b], later_shares[:, a:b], MULT)
         nc.vector.tensor_tensor(
-            mem_t[:].indirect(entries(slot_t, CHUNK, S)), later_scaled[:, 0, :], later_scaled[:, 1, :], ADD
+            mem_t[:].indirect(entries(slot_t, CHUNK, S)), later_scaled[:, : S - CHUNK], later_scaled[:, S - CHUNK :], ADD
         )
         nc.sync.dma_start(out=out, in_=mem_t[:])

@@ -90,7 +90,10 @@ def tile_picked_ema_tanh_e_kernel(
 
         def weave(z, a, b):
             woven = sb.tile([P, b - a, PACK], BF16, name="woven%d_%d" % (z, a), align_bytes=64)
-            nc.vector.tensor_copy(woven[:], picked[z][:, :, a:b].rearrange("p t j -> p j t"))
+            nc.vector.tensor_copy(
+                woven[:].rearrange("p (c i) t -> p c t i", i=PACK),
+                picked[z][:, :, a:b].rearrange("p t (c i) -> p c t i", i=PACK),
+            )
             return woven[:]
 
         def quantise(woven, name, tag):
@@ -146,19 +149,19 @@ def tile_picked_ema_tanh_e_kernel(
         woven2 = weave(1, *PARTS[2])
         second_pass(1, first_woven[:, CHUNK:, :], "codes1_1")
         second_pass(2, woven2, "codes1_2")
-        first_terms = sb.tile([P, 2, CHUNK], F32, name="first_terms")
-        nc.scalar.activation(first_terms[:, 1, :], mem_t[:].indirect(entries(slot_t, 0, CHUNK)), COPY)
+        first_terms = sb.tile([P, 3, CHUNK], F32, name="first_terms")
+        nc.scalar.activation(
+            first_terms[:, 1:, :].rearrange("p i j -> p (i j)"), mem_t[:].indirect(entries(slot_t, 0, HALF)), COPY
+        )
         nc.scalar.activation(first_terms[:, 0, :], accs[0][:], TANH)
         later_terms = sb.tile([P, HALF + S - CHUNK], F32, name="later_terms", tag="ring", align_bytes=64)
         nc.scalar.activation(later_terms[:, :HALF], mem_t[:].indirect(entries(slot_t, HALF, S)), COPY)
         nc.scalar.activation(later_terms[:, HALF : HALF + CHUNK], accs[1][:], TANH)
         nc.scalar.activation(later_terms[:, HALF + CHUNK :], accs[2][:], TANH)
         first_scaled = sb.tile([P, 2, CHUNK], F32, name="first_scaled")
-        nc.vector.tensor_tensor(first_scaled[:], first_terms[:], first_shares[:, :2, :], MULT)
+        nc.vector.tensor_tensor(first_scaled[:], first_terms[:, :2, :], first_shares[:, :2, :], MULT)
         later_scaled = sb.tile([P, 2 * (S - CHUNK)], F32, name="later_scaled")
-        nc.vector.tensor_tensor(
-            later_scaled[:, :CHUNK], mem_t[:].indirect(entries(slot_t, CHUNK, HALF)), first_shares[:, 2, :], MULT
-        )
+        nc.vector.tensor_tensor(later_scaled[:, :CHUNK], first_terms[:, 2, :], first_shares[:, 2, :], MULT)
         first_total = sb.tile([P, CHUNK], F32, name="first_total")
         nc.vector.tensor_tensor(first_total[:], first_scaled[:, 0, :], first_scaled[:, 1, :], ADD)
         nc.scalar.activation(mem_t[:].indirect(entries(slot_t, 0, CHUNK)), first_total[:], COPY)

@@ -22,6 +22,7 @@ PASSES = 2
 PACK = 4
 CHUNK = 128
 HALF = S // 2
+FILL = 64
 PARTS = [(0, CHUNK), (CHUNK, HALF), (HALF, S)]
 
 
@@ -88,12 +89,15 @@ def tile_picked_ema_tanh_e_kernel(
         def pick_woven(r, a, b):
             nc.vector.tensor_copy(first_woven[:, a:b, r % PACK], rows[r][:].indirect(entries(offs_t, a, b)))
 
-        def weave(z, a, b):
-            woven = sb.tile([P, b - a, PACK], BF16, name="woven%d_%d" % (z, a), align_bytes=64)
-            nc.vector.tensor_copy(
-                woven[:].rearrange("p (c i) t -> p c t i", i=PACK),
+        def weave_into(copy, woven, z, a, b):
+            copy(
+                woven.rearrange("p (c i) t -> p c t i", i=PACK),
                 picked[z][:, :, a:b].rearrange("p t (c i) -> p c t i", i=PACK),
             )
+
+        def weave(z, a, b):
+            woven = sb.tile([P, b - a, PACK], BF16, name="woven%d_%d" % (z, a), align_bytes=64)
+            weave_into(nc.vector.tensor_copy, woven[:], z, a, b)
             return woven[:]
 
         def quantise(woven, name, tag):
@@ -136,7 +140,10 @@ def tile_picked_ema_tanh_e_kernel(
         nc.vector.tensor_copy(first_woven[:, :, :2], picked[1][:, :2, :HALF].rearrange("p t j -> p j t"))
         pick_scalar(6, HALF, S)
         pick_woven(6, 0, HALF)
-        pick_scalar(7, HALF, S)
+        pick_scalar(7, S - CHUNK, S)
+        pick_scalar(7, HALF, S - CHUNK)
+        woven2 = sb.tile([P, HALF, PACK], BF16, name="woven2", align_bytes=64)
+        weave_into(nc.scalar.copy, woven2[:, CHUNK:, :], 1, S - CHUNK, S)
         for a, b in PARTS[:2]:
             pick_woven(7, a, b)
 
@@ -146,16 +153,17 @@ def tile_picked_ema_tanh_e_kernel(
             product(accs[c], 1, codes[:], scales[:])
 
         second_pass(0, first_woven[:, :CHUNK, :], "ring")
-        woven2 = weave(1, *PARTS[2])
+        weave_into(nc.vector.tensor_copy, woven2[:, :CHUNK, :], 1, HALF, S - CHUNK)
         second_pass(1, first_woven[:, CHUNK:, :], "codes1_1")
-        second_pass(2, woven2, "codes1_2")
+        second_pass(2, woven2[:], "codes1_2")
         first_terms = sb.tile([P, 3, CHUNK], F32, name="first_terms")
         nc.scalar.activation(
             first_terms[:, 1:, :].rearrange("p i j -> p (i j)"), mem_t[:].indirect(entries(slot_t, 0, HALF)), COPY
         )
         nc.scalar.activation(first_terms[:, 0, :], accs[0][:], TANH)
         later_terms = sb.tile([P, HALF + S - CHUNK], F32, name="later_terms", tag="ring", align_bytes=64)
-        nc.scalar.activation(later_terms[:, :HALF], mem_t[:].indirect(entries(slot_t, HALF, S)), COPY)
+        nc.vector.tensor_copy(later_terms[:, :FILL], mem_t[:].indirect(entries(slot_t, HALF, HALF + FILL)))
+        nc.scalar.activation(later_terms[:, FILL:HALF], mem_t[:].indirect(entries(slot_t, HALF + FILL, S)), COPY)
         nc.scalar.activation(later_terms[:, HALF : HALF + CHUNK], accs[1][:], TANH)
         nc.scalar.activation(later_terms[:, HALF + CHUNK :], accs[2][:], TANH)
         first_scaled = sb.tile([P, 2, CHUNK], F32, name="first_scaled")

@@ -23,6 +23,7 @@ PACK = 4
 CHUNK = 128
 HALF = S // 2
 FILL = 64
+BURST = 256
 PARTS = [(0, CHUNK), (CHUNK, HALF), (HALF, S)]
 
 
@@ -36,10 +37,10 @@ def tile_picked_ema_tanh_e_kernel(
 
         offs_t = sb.tile([P, S // 16], U16, name="offs_t")
         slot_t = sb.tile([P, S // 16], U16, name="slot_t")
-        mem_t = sb.tile([P, U], F32, name="mem_t")
-        first_shares = sb.tile([P, 3, CHUNK], F32, name="first_shares")
-        later_shares = sb.tile([P, HALF + S - CHUNK], F32, name="later_shares")
-        w_words = [sb.tile([P, N], U32, name="w_words%d" % z, align_bytes=64) for z in range(PASSES)]
+        mem_t = sb.tile([P, U], F32, name="mem_t", align_bytes=BURST)
+        first_shares = sb.tile([P, 3, CHUNK], F32, name="first_shares", align_bytes=BURST)
+        later_shares = sb.tile([P, HALF + S - CHUNK], F32, name="later_shares", align_bytes=BURST)
+        w_words = [sb.tile([P, N], U32, name="w_words%d" % z, align_bytes=BURST) for z in range(PASSES)]
         w_scales = sb.tile([P, PASSES, N], U8, name="w_scales", align_bytes=64)
 
         nc.vector.memset(w_scales[:].bitcast(I32), 0)
@@ -57,7 +58,7 @@ def tile_picked_ema_tanh_e_kernel(
             )
 
         x_rows = xT.rearrange("(z p t) c -> z t p c", z=PASSES, p=P, t=PACK)
-        rows = [sb.tile([P, T], F32, name="row%d" % r) for r in range(PASSES * PACK)]
+        rows = [sb.tile([P, T], F32, name="row%d" % r, align_bytes=BURST) for r in range(PASSES * PACK)]
         for r in range(PASSES * PACK):
             nc.sync.dma_start(out=rows[r][:], in_=x_rows[r // PACK, r % PACK])
             if r == 0:

@@ -22,7 +22,6 @@ PASSES = 2
 PACK = 4
 CHUNK = 128
 HALF = S // 2
-FILL = 64
 BURST = 256
 PARTS = [(0, CHUNK), (CHUNK, HALF), (HALF, S)]
 
@@ -38,8 +37,9 @@ def tile_picked_ema_tanh_e_kernel(
         offs_t = sb.tile([P, S // 16], U16, name="offs_t")
         slot_t = sb.tile([P, S // 16], U16, name="slot_t")
         mem_t = sb.tile([P, U], F32, name="mem_t", align_bytes=BURST)
-        first_shares = sb.tile([P, 3, CHUNK], F32, name="first_shares", align_bytes=BURST)
-        later_shares = sb.tile([P, HALF + S - CHUNK], F32, name="later_shares", align_bytes=BURST)
+        terms = sb.tile([P, 3, CHUNK], F32, name="terms", align_bytes=BURST)
+        later_old = sb.tile([P, S - CHUNK], F32, name="later_old", align_bytes=BURST)
+        later_new = sb.tile([P, S - CHUNK], F32, name="later_new", align_bytes=BURST)
         w_words = [sb.tile([P, N], U32, name="w_words%d" % z, align_bytes=BURST) for z in range(PASSES)]
         w_scales = sb.tile([P, PASSES, N], U8, name="w_scales", align_bytes=64)
 
@@ -68,12 +68,12 @@ def tile_picked_ema_tanh_e_kernel(
             if r == 5:
                 nc.sync.dma_start(slot_t[:], slot)
         load_weights(0)
-        nc.sync.dma_start(out=mem_t[:], in_=mem)
         load_weights(1)
-        nc.sync.dma_start(out=first_shares[:, 0, :], in_=new[:, :CHUNK])
-        nc.sync.dma_start(out=first_shares[:, 1:, :].rearrange("p i j -> p (i j)"), in_=old[:, :HALF])
-        nc.sync.dma_start(out=later_shares[:, :HALF], in_=old[:, HALF:])
-        nc.sync.dma_start(out=later_shares[:, HALF:], in_=new[:, CHUNK:])
+        nc.sync.dma_start(out=mem_t[:], in_=mem)
+        nc.sync.dma_start(out=terms[:, 2, :], in_=old[:, :CHUNK])
+        nc.sync.dma_start(out=terms[:, 1, :], in_=new[:, :CHUNK])
+        nc.sync.dma_start(out=later_old[:], in_=old[:, CHUNK:])
+        nc.sync.dma_start(out=later_new[:], in_=new[:, CHUNK:])
 
         picked = [sb.tile([P, PACK, S], BF16, name="picked%d" % z, align_bytes=64) for z in range(PASSES)]
         first_woven = sb.tile([P, HALF, PACK], BF16, name="first_woven", align_bytes=64)
@@ -112,15 +112,15 @@ def tile_picked_ema_tanh_e_kernel(
             )
             return codes, scales
 
-        def product(acc, z, codes, scales):
+        def product(acc, z, codes, scales, stop):
             nc.tensor.matmul_mx(
-                out=acc[:],
+                out=acc,
                 lhsT=w_words[z][:].bitcast(FP8X4),
                 lhsT_scale=w_scales[:, z, :],
                 rhs=codes.bitcast(FP8X4),
                 rhs_scale=scales,
                 start=(z == 0),
-                stop=(z == PASSES - 1),
+                stop=stop,
             )
 
         accs = [ps.tile([P, b - a], F32, name="acc%d" % a) for a, b in PARTS]
@@ -141,42 +141,40 @@ def tile_picked_ema_tanh_e_kernel(
         nc.vector.tensor_copy(first_woven[:, :, :2], picked[1][:, :2, :HALF].rearrange("p t j -> p j t"))
         pick_scalar(6, HALF, S)
         pick_woven(6, 0, HALF)
-        pick_scalar(7, S - CHUNK, S)
-        pick_scalar(7, HALF, S - CHUNK)
         woven2 = sb.tile([P, HALF, PACK], BF16, name="woven2", align_bytes=64)
+        pick_scalar(7, HALF, S - CHUNK)
+        pick_scalar(7, S - CHUNK, S)
+        pick_scalar(7, CHUNK, HALF)
         weave_into(nc.scalar.copy, woven2[:, CHUNK:, :], 1, S - CHUNK, S)
-        for a, b in PARTS[:2]:
-            pick_woven(7, a, b)
+        pick_woven(7, 0, CHUNK)
+        for c in range(len(PARTS)):
+            product(accs[c][:], 0, *first_pass[c], False)
 
-        def second_pass(c, woven, tag):
-            codes, scales = quantise(woven, "1_%d" % c, tag)
-            product(accs[c], 0, *first_pass[c])
-            product(accs[c], 1, codes[:], scales[:])
+        def second_pass(c, woven, acc, stop):
+            codes, scales = quantise(woven, "1_%d" % c, "codes1_%d" % c)
+            product(acc, 1, codes[:], scales[:], stop)
 
-        second_pass(0, first_woven[:, :CHUNK, :], "ring")
+        second_pass(0, first_woven[:, :CHUNK, :], accs[0][:], True)
         weave_into(nc.vector.tensor_copy, woven2[:, :CHUNK, :], 1, HALF, S - CHUNK)
-        second_pass(1, first_woven[:, CHUNK:, :], "codes1_1")
-        second_pass(2, woven2[:], "codes1_2")
-        first_terms = sb.tile([P, 3, CHUNK], F32, name="first_terms")
-        nc.scalar.activation(
-            first_terms[:, 1:, :].rearrange("p i j -> p (i j)"), mem_t[:].indirect(entries(slot_t, 0, HALF)), COPY
-        )
-        nc.scalar.activation(first_terms[:, 0, :], accs[0][:], TANH)
-        later_terms = sb.tile([P, HALF + S - CHUNK], F32, name="later_terms", tag="ring", align_bytes=64)
-        nc.vector.tensor_copy(later_terms[:, :FILL], mem_t[:].indirect(entries(slot_t, HALF, HALF + FILL)))
-        nc.scalar.activation(later_terms[:, FILL:HALF], mem_t[:].indirect(entries(slot_t, HALF + FILL, S)), COPY)
-        nc.scalar.activation(later_terms[:, HALF : HALF + CHUNK], accs[1][:], TANH)
-        nc.scalar.activation(later_terms[:, HALF + CHUNK :], accs[2][:], TANH)
+        nc.vector.tensor_copy(first_woven[:, CHUNK:, PACK - 1], picked[1][:, PACK - 1, CHUNK:HALF])
+        second_pass(2, woven2[:, :CHUNK, :], accs[2][:, :CHUNK], False)
+        second_pass(1, first_woven[:, CHUNK:, :], accs[1][:], True)
+        second_pass(3, woven2[:, CHUNK:, :], accs[2][:, CHUNK:], True)
+        nc.scalar.activation(terms[:, 0, :], accs[0][:], TANH)
+        later_mem = sb.tile([P, S - CHUNK], F32, name="later_mem")
+        nc.scalar.activation(later_mem[:], mem_t[:].indirect(entries(slot_t, CHUNK, S)), COPY)
         first_scaled = sb.tile([P, 2, CHUNK], F32, name="first_scaled")
-        nc.vector.tensor_tensor(first_scaled[:], first_terms[:, :2, :], first_shares[:, :2, :], MULT)
-        later_scaled = sb.tile([P, 2 * (S - CHUNK)], F32, name="later_scaled")
-        nc.vector.tensor_tensor(later_scaled[:, :CHUNK], first_terms[:, 2, :], first_shares[:, 2, :], MULT)
+        nc.vector.tensor_tensor(first_scaled[:, 0, :], mem_t[:].indirect(entries(slot_t, 0, CHUNK)), terms[:, 2, :], MULT)
+        nc.vector.tensor_tensor(first_scaled[:, 1, :], terms[:, 0, :], terms[:, 1, :], MULT)
+        nc.scalar.activation(terms[:, 0, :], accs[1][:], TANH)
+        nc.scalar.activation(terms[:, 1:, :].rearrange("p i j -> p (i j)"), accs[2][:], TANH)
         first_total = sb.tile([P, CHUNK], F32, name="first_total")
         nc.vector.tensor_tensor(first_total[:], first_scaled[:, 0, :], first_scaled[:, 1, :], ADD)
         nc.scalar.activation(mem_t[:].indirect(entries(slot_t, 0, CHUNK)), first_total[:], COPY)
-        for a, b in ((0, HALF + CHUNK), (HALF + CHUNK, HALF + S - CHUNK)):
-            nc.vector.tensor_tensor(later_scaled[:, CHUNK + a : CHUNK + b], later_terms[:, a:b], later_shares[:, a:b], MULT)
+        later_scaled = sb.tile([P, 2, S - CHUNK], F32, name="later_scaled")
+        nc.vector.tensor_tensor(later_scaled[:, 0, :], later_mem[:], later_old[:], MULT)
+        nc.vector.tensor_tensor(later_scaled[:, 1, :], terms[:].rearrange("p i j -> p (i j)"), later_new[:], MULT)
         nc.vector.tensor_tensor(
-            mem_t[:].indirect(entries(slot_t, CHUNK, S)), later_scaled[:, : S - CHUNK], later_scaled[:, S - CHUNK :], ADD
+            mem_t[:].indirect(entries(slot_t, CHUNK, S)), later_scaled[:, 0, :], later_scaled[:, 1, :], ADD
         )
         nc.sync.dma_start(out=out, in_=mem_t[:])

@@ -65,10 +65,9 @@ def tile_picked_ema_tanh_e_kernel(
                 nc.sync.dma_start(offs_t[:], offs)
             if 1 <= r < 5:
                 load_scale_rows(r - 1)
-            if r == 5:
-                nc.sync.dma_start(slot_t[:], slot)
         load_weights(0)
         load_weights(1)
+        nc.sync.dma_start(slot_t[:], slot)
         nc.sync.dma_start(out=mem_t[:], in_=mem)
         nc.sync.dma_start(out=terms[:, 2, :], in_=old[:, :CHUNK])
         nc.sync.dma_start(out=terms[:, 1, :], in_=new[:, :CHUNK])

from contextlib import ExitStack

import concourse.mybir as mybir

K, T, S, N, U = 1024, 1024, 512, 128, 1024
FLOPS = 2 * K * N * S

F32 = mybir.dt.float32
BF16 = mybir.dt.bfloat16
I32 = mybir.dt.int32
U32 = mybir.dt.uint32
U16 = mybir.dt.uint16
U8 = mybir.dt.uint8
FP8X4 = mybir.dt.float8_e4m3fn_x4
MULT = mybir.AluOpType.mult
ADD = mybir.AluOpType.add
TANH = mybir.ActivationFunctionType.Tanh
COPY = mybir.ActivationFunctionType.Copy

P = 128
PASSES = 2
PACK = 4
CHUNK = 128
HALF = S // 2
BURST = 256
PARTS = [(0, CHUNK), (CHUNK, HALF), (HALF, S)]


def tile_picked_ema_tanh_e_kernel(
    tc, xT, mem, w1_words, w1_scales, old, new, offs, slot, out
):
    nc = tc.nc
    with ExitStack() as ctx:
        sb = ctx.enter_context(tc.tile_pool(name="sb", bufs=1))
        ps = ctx.enter_context(tc.psum_pool(name="ps", bufs=1))

        offs_t = sb.tile([P, S // 16], U16, name="offs_t")
        slot_t = sb.tile([P, S // 16], U16, name="slot_t")
        mem_t = sb.tile([P, U], F32, name="mem_t", align_bytes=BURST)
        terms = sb.tile([P, 3, CHUNK], F32, name="terms", align_bytes=BURST)
        later_old = sb.tile([P, S - CHUNK], F32, name="later_old", align_bytes=BURST)
        later_new = sb.tile([P, S - CHUNK], F32, name="later_new", align_bytes=BURST)
        w_words = [sb.tile([P, N], U32, name="w_words%d" % z, align_bytes=BURST) for z in range(PASSES)]
        w_scales = sb.tile([P, PASSES, N], U8, name="w_scales", align_bytes=64)

        nc.vector.memset(w_scales[:].bitcast(I32), 0)

        def load_scale_rows(q):
            nc.sync.dma_start(
                out=w_scales[32 * q : 32 * q + 4, :, :].bitcast(I32),
                in_=w1_scales[:, 4 * q : 4 * q + 4, :].rearrange("z r n -> r z n").bitcast(I32),
            )

        def load_weights(z):
            nc.sync.dma_start(
                out=w_words[z][:].bitcast(I32),
                in_=w1_words[z].rearrange("p n t -> p (n t)").bitcast(I32),
            )

        x_rows = xT.rearrange("(z p t) c -> z t p c", z=PASSES, p=P, t=PACK)
        rows = [sb.tile([P, T], F32, name="row%d" % r, align_bytes=BURST) for r in range(PASSES * PACK)]
        for r in range(PASSES * PACK):
            nc.sync.dma_start(out=rows[r][:], in_=x_rows[r // PACK, r % PACK])
            if r == 0:
                nc.sync.dma_start(offs_t[:], offs)
            if 1 <= r < 5:
                load_scale_rows(r - 1)
        load_weights(0)
        load_weights(1)
        nc.sync.dma_start(slot_t[:], slot)
        nc.sync.dma_start(out=mem_t[:], in_=mem)
        nc.sync.dma_start(out=terms[:, 2, :], in_=old[:, :CHUNK])
        nc.sync.dma_start(out=terms[:, 1, :], in_=new[:, :CHUNK])
        nc.sync.dma_start(out=later_old[:], in_=old[:, CHUNK:])
        nc.sync.dma_start(out=later_new[:], in_=new[:, CHUNK:])

        picked = [sb.tile([P, PACK, S], BF16, name="picked%d" % z, align_bytes=64) for z in range(PASSES)]
        first_woven = sb.tile([P, HALF, PACK], BF16, name="first_woven", align_bytes=64)

        def entries(listed, a, b):
            return listed[:, a // 16 : b // 16]

        def pick_scalar(r, a, b):
            nc.scalar.activation(picked[r // PACK][:, r % PACK, a:b], rows[r][:].indirect(entries(offs_t, a, b)), COPY)

        def pick_vector(r, a, b):
            nc.vector.tensor_copy(picked[r // PACK][:, r % PACK, a:b], rows[r][:].indirect(entries(offs_t, a, b)))

        def pick_woven(r, a, b):
            nc.vector.tensor_copy(first_woven[:, a:b, r % PACK], rows[r][:].indirect(entries(offs_t, a, b)))

        def weave_into(copy, woven, z, a, b):
            copy(
                woven.rearrange("p (c i) t -> p c t i", i=PACK),
                picked[z][:, :, a:b].rearrange("p t (c i) -> p c t i", i=PACK),
            )

        def weave(z, a, b):
            woven = sb.tile([P, b - a, PACK], BF16, name="woven%d_%d" % (z, a), align_bytes=64)
            weave_into(nc.vector.tensor_copy, woven[:], z, a, b)
            return woven[:]

        def quantise(woven, name, tag):
            width = woven.shape[1]
            codes = sb.tile([P, width], U32, name="codes" + name, tag=tag, align_bytes=64)
            scales = sb.tile([P, width], U8, name="scales" + name, align_bytes=64)
            nc.vector.quantize_mx(
                out=codes[:].bitcast(FP8X4),
                scales=scales[:],
                in_=woven.rearrange("p j t -> p (j t)"),
            )
            return codes, scales

        def product(acc, z, codes, scales, stop):
            nc.tensor.matmul_mx(
                out=acc,
                lhsT=w_words[z][:].bitcast(FP8X4),
                lhsT_scale=w_scales[:, z, :],
                rhs=codes.bitcast(FP8X4),
                rhs_scale=scales,
                start=(z == 0),
                stop=stop,
            )

        accs = [ps.tile([P, b - a], F32, name="acc%d" % a) for a, b in PARTS]

        pick_scalar(0, 0, S)
        pick_vector(1, 0, S)
        for r in (2, 3):
            pick_scalar(r, 0, HALF)
            pick_vector(r, HALF, S)
        halves = [weave(0, 0, HALF), weave(0, HALF, S)]
        codes, scales = quantise(halves[0], "0_0", "codes0_0")
        first_pass = [(codes[:, a:b], scales[:, a:b]) for a, b in PARTS[:2]]
        codes, scales = quantise(halves[1], "0_1", "codes0_1")
        first_pass.append((codes[:], scales[:]))
        pick_scalar(4, 0, S)
        pick_scalar(5, 0, HALF)
        pick_scalar(5, HALF, S)
        nc.vector.tensor_copy(first_woven[:, :, :2], picked[1][:, :2, :HALF].rearrange("p t j -> p j t"))
        pick_scalar(6, HALF, S)
        pick_woven(6, 0, HALF)
        woven2 = sb.tile([P, HALF, PACK], BF16, name="woven2", align_bytes=64)
        pick_scalar(7, HALF, S - CHUNK)
        pick_scalar(7, S - CHUNK, S)
        pick_scalar(7, CHUNK, HALF)
        weave_into(nc.scalar.copy, woven2[:, CHUNK:, :], 1, S - CHUNK, S)
        pick_woven(7, 0, CHUNK)
        for c in range(len(PARTS)):
            product(accs[c][:], 0, *first_pass[c], False)

        def second_pass(c, woven, acc, stop):
            codes, scales = quantise(woven, "1_%d" % c, "codes1_%d" % c)
            product(acc, 1, codes[:], scales[:], stop)

        second_pass(0, first_woven[:, :CHUNK, :], accs[0][:], True)
        weave_into(nc.vector.tensor_copy, woven2[:, :CHUNK, :], 1, HALF, S - CHUNK)
        nc.vector.tensor_copy(first_woven[:, CHUNK:, PACK - 1], picked[1][:, PACK - 1, CHUNK:HALF])
        second_pass(2, woven2[:, :CHUNK, :], accs[2][:, :CHUNK], False)
        second_pass(1, first_woven[:, CHUNK:, :], accs[1][:], True)
        second_pass(3, woven2[:, CHUNK:, :], accs[2][:, CHUNK:], True)
        nc.scalar.activation(terms[:, 0, :], accs[0][:], TANH)
        later_mem = sb.tile([P, S - CHUNK], F32, name="later_mem")
        nc.scalar.activation(later_mem[:], mem_t[:].indirect(entries(slot_t, CHUNK, S)), COPY)
        first_scaled = sb.tile([P, 2, CHUNK], F32, name="first_scaled")
        nc.vector.tensor_tensor(first_scaled[:, 0, :], mem_t[:].indirect(entries(slot_t, 0, CHUNK)), terms[:, 2, :], MULT)
        nc.vector.tensor_tensor(first_scaled[:, 1, :], terms[:, 0, :], terms[:, 1, :], MULT)
        nc.scalar.activation(terms[:, 0, :], accs[1][:], TANH)
        nc.scalar.activation(terms[:, 1:, :].rearrange("p i j -> p (i j)"), accs[2][:], TANH)
        first_total = sb.tile([P, CHUNK], F32, name="first_total")
        nc.vector.tensor_tensor(first_total[:], first_scaled[:, 0, :], first_scaled[:, 1, :], ADD)
        nc.scalar.activation(mem_t[:].indirect(entries(slot_t, 0, CHUNK)), first_total[:], COPY)
        later_scaled = sb.tile([P, 2, S - CHUNK], F32, name="later_scaled")
        nc.vector.tensor_tensor(later_scaled[:, 0, :], later_mem[:], later_old[:], MULT)
        nc.vector.tensor_tensor(later_scaled[:, 1, :], terms[:].rearrange("p i j -> p (i j)"), later_new[:], MULT)
        nc.vector.tensor_tensor(
            mem_t[:].indirect(entries(slot_t, CHUNK, S)), later_scaled[:, 0, :], later_scaled[:, 1, :], ADD
        )
        nc.sync.dma_start(out=out, in_=mem_t[:])
